import numpy as np
CORES = [16,17,18,19,150,151]
N = 6
R, L = 4096, 1024
CAPP = 512
def entries(a): return a.T.reshape(-1)
def pack(v, P): return np.ascontiguousarray(np.asarray(v, np.int32).reshape(-1, P).T)
def lists(rng, how):
    n = N * L
    P = rng.permutation(np.repeat(np.arange(N * N), CAPP))[:n]
    if how == "full":
        a, b = rng.permutation(N)[:2]; o = rng.permutation(N * N); o = o[(o // N != a) & (o % N != b)]
        C = np.concatenate([N * a + rng.permutation(np.delete(np.arange(N), b)), [N * a + b], N * rng.permutation(np.delete(np.arange(N), a)) + b, o])[:n // CAPP]
        P = np.repeat(C, CAPP).reshape(N, L)[rng.permutation(N)].reshape(-1)
    h, g = P // N, P % N
    d = np.zeros(n, np.int64)
    for q in range(N): m = np.nonzero(g == q)[0]; d[m] = R * q + np.concatenate([[0, R - 1], 1 + rng.permutation(R - 2)])[:len(m)]
    s = R * h + rng.integers(0, R, n)
    if how == "fork": s = R * h + rng.integers(0, R, N)[h]
    if how == "chain":
        for q in range(N):
            m = np.nonzero(h == q)[0]; w = d[g == q]
            if len(w): s[m] = w[rng.integers(0, len(w), len(m))]
    if how == "gaps":
        z = rng.permutation(N)[:3]; k = (rng.random(n) < 0.5) | (np.arange(n) // L == z[0]) | (h == z[1]) | (g == z[2]); s[k] = -1; d[k] = -1
    return {"src": np.stack([pack(v, 16) for v in s.reshape(N, L)]), "dst": np.stack([pack(v, 16) for v in d.reshape(N, L)])}
def setup_inputs(rng):
    return dict({"tab": rng.standard_normal((N, 128, R), dtype=np.float32)}, **lists(rng, "uniform"))
def setup_inputs_chain(rng):
    d = setup_inputs(rng); d.update(lists(rng, "chain"))
    for k in ("tab",): d[k] = (d[k].astype(np.float32) * 1048576.0).astype(d[k].dtype)
    return d
def setup_inputs_fork(rng):
    d = setup_inputs(rng); d.update(lists(rng, "fork"))
    for k in ("tab",): d[k] = (d[k].astype(np.float32) * (1 / 1024.0)).astype(d[k].dtype)
    return d
def setup_inputs_full(rng):
    d = setup_inputs(rng); d.update(lists(rng, "full"))
    return d
def setup_inputs_gaps(rng):
    d = setup_inputs(rng); d.update(lists(rng, "gaps"))
    return d
def check_inputs(x):
    bad = []; s, d = x["src"].reshape(-1), x["dst"].reshape(-1); k = d >= 0
    if s.min() < -1 or s.max() >= N * R or d.min() < -1 or d.max() >= N * R: bad.append("out of range")
    if ((s < 0) != (d < 0)).any(): bad.append("half a pair")
    if len(np.unique(d[k])) != int(k.sum()): bad.append("a column is written twice")
    if k.any() and int(np.bincount(s[k] // R * N + d[k] // R).max()) > CAPP: bad.append("more than CAPP pairs from one rank's part to one rank's part")
    return bad
def reference(tab, src, dst):
    A = np.concatenate(list(tab), axis=1); Y = A.copy()
    for r in range(N):
        s, d = entries(src[r]), entries(dst[r]); k = d >= 0
        Y[:, d[k]] = A[:, s[k]]
    return {"y": np.stack([Y[:, R * r:R * r + R] for r in range(N)])}

@@ -1,0 +1,447 @@
+from concourse.bass import DstId, RemoteDMATransfer
+from concourse.mybir import AluOpType, ActivationFunctionType
+
+N, R, L, CAPP = 6, 4096, 1024, 512
+SIM_CORES = 256
+LT = L // 128
+NT = N * LT
+CW = NT + 1
+MW = N * CW
+CWE = LT + 1
+MWE = N * CWE
+Q = 16
+MS = CAPP // Q
+PR = 192
+MID = R // 2
+GAP = 4
+WIN = R + N * CAPP + GAP
+YBLOCKS = [512, 1024, 1024, 1024, 512]
+
+
+def sbuf(dtype, *shape):
+    return ("sbuf", [128] + list(shape), dtype)
+
+
+SCRATCH = {
+    "LAND": sbuf("int32", N, 2 * LT),
+    "M": sbuf("bfloat16", MW), "RST": sbuf("float32", MW), "ME": sbuf("bfloat16", MWE), "RSTE": sbuf("float32", MWE),
+    "M2": sbuf("bfloat16", MW), "BASE": sbuf("bfloat16", MW), "ONE": sbuf("bfloat16", 128),
+    "U": sbuf("bfloat16", 128), "U2": sbuf("bfloat16", 128), "SEL": sbuf("bfloat16", 8 * 128),
+    "MZ": sbuf("float32", MW), "R1": sbuf("float32", 3 * CW), "R2": sbuf("float32", NT),
+    "SH": sbuf("int32", NT), "DH": sbuf("int32", NT), "LOW": sbuf("int32", NT), "POSI": sbuf("int32", NT),
+    "REM": sbuf("int32", NT), "NM": sbuf("float32", NT), "X": sbuf("float32", NT), "X16": sbuf("float32", NT),
+    "KEY": sbuf("float32", NT), "VAL": sbuf("float32", NT),
+    "POSE": sbuf("float32", LT), "POS": sbuf("float32", NT), "DLF": sbuf("float32", NT),
+    "IOT": sbuf("bfloat16", 128), "CB": sbuf("float32", MS + 1), "CB2": sbuf("float32", MS + 1),
+    "C16": sbuf("bfloat16", MS + 1), "C128": sbuf("bfloat16", MS + 1),
+    "FH": sbuf("bfloat16", R // Q), "FL": sbuf("bfloat16", R // Q), "KD": sbuf("float32", R // Q),
+    "NZ": sbuf("float32", 1),
+    "A1": sbuf("float16", NT, N * Q), "A2": sbuf("float16", NT, 128),
+    "B1": sbuf("bfloat16", NT, MS + 2), "B2": sbuf("bfloat16", NT, MS + 2),
+    "OC": sbuf("float32", MS), "DIF": sbuf("float16", MS), "ADD": sbuf("float32", R // Q),
+    "OFS": sbuf("uint16", N * MS), "INV": sbuf("uint16", R // Q),
+    "TW": sbuf("float32", WIN), "SEND": sbuf("float32", N, CAPP), "YB": sbuf("float32", R),
+    "RB": sbuf("float32", 2, PR),
+}
+for _k in ("PINC", "PZ", "PO", "PWO", "PWN", "PO2", "PW2"):
+    SCRATCH[_k] = ("psum", [128, 512], "float32")
+SEMAPHORES = (["ld", "tl", "la", "sn", "sx", "st", "gs", "vs", "acs", "ps", "rl0", "rl1"]
+              + ["r%s%d" % (p, a) for p in "abc" for a in range(N)])
+
+
+def same_chip(topo, a, b):
+    return topo.host(a) == topo.host(b) and topo.chip(a) == topo.chip(b)
+
+
+def others(T, topo, rank):
+    c = T.cores[rank]
+    off = [d for d in range(N) if not same_chip(topo, T.cores[d], c)]
+    on = [d for d in range(N) if d != rank and d not in off]
+    return off, on
+
+
+def relays(T, topo, rank):
+    c = T.cores[rank]
+    peers = [x for x in T.cores if same_chip(topo, x, c)]
+    cand = [x for x in range(SIM_CORES) if same_chip(topo, x, c) and topo.die(x) != topo.die(c) and x not in T.cores]
+    off, _ = others(T, topo, rank)
+    k = len(cand) // len(peers)
+    i = peers.index(c)
+    mine = cand[i * k:(i + 1) * k]
+    m = len(off) // k
+    return [(mine[j], off[j * m:(j + 1) * m]) for j in range(k)]
+
+
+def bits(mask):
+    return [1 << i for i in range(16) if (mask >> i) & 1]
+
+
+def split(mask, n):
+    b = bits(mask)
+    k = 1
+    while 2 * k * n <= len(b):
+        k *= 2
+    return [sum(b[j * k:(j + 1) * k]) for j in range(n)], k
+
+
+def portions(items):
+    out, todo = [], list(items)
+    while todo:
+        n = 1
+        while 2 * n <= len(todo):
+            n *= 2
+        out.append(todo[:n])
+        todo = todo[n:]
+    return out
+
+
+def place(r, c):
+    return (c - r) % N
+
+
+def runs(r, a):
+    d = (a - r) % N
+    return [(0, d, N - d), (N - d, 0, d)] if d else [(0, 0, N)]
+
+
+def landed(a):
+    return R + a * CAPP + (GAP if a * CAPP >= MID else 0)
+
+
+def dst_id(topo, dst, src):
+    rid, pid = topo.addr(dst, src)
+    return DstId(rid=rid, pnc=pid)
+
+
+def relay_program(g, core, T, topo):
+    for rank in range(N):
+        for c, dests in relays(T, topo, rank):
+            if c != core:
+                continue
+            src = T.cores[rank]
+            off, _ = others(T, topo, rank)
+            inside = topo.mask(src, core) & ~topo.mask(src, T.cores[off[0]])
+            _, k = split(inside, len(relays(T, topo, rank)))
+            masks, kk = split(topo.mask(core, T.cores[dests[0]]), len(dests))
+            to = landed(rank)
+            for j, d in enumerate(dests):
+                g.wait_ge(T.sem["rl%d" % j], k)
+                g.remote_dma_fused([RemoteDMATransfer(dst_ids=[dst_id(topo, T.cores[d], core)], dma_engine_mask=masks[j],
+                                                      remote_sem=T.sem["ra%d" % rank], src=T.RB[:, j, :],
+                                                      dst=T.TW[:, to:to + PR])], local_sem=T.sem.sx)
+            g.wait_ge(T.sem.sx, kk * len(dests))
+
+
+def rank_program(g, core, T, topo):
+    me = T.rank_of(core)
+    if me is None:
+        return relay_program(g, core, T, topo)
+    op, fn = AluOpType, ActivationFunctionType
+    off, on = others(T, topo, me)
+    outside = topo.mask(core, T.cores[off[0]])
+    inside = topo.mask(core, T.cores[on[0]]) & ~outside
+    queue = {"g": g, "v": g.vector, "a": g.scalar, "p": g.tensor, "s": g.sync}
+    count = {"gs": 0, "vs": 0, "acs": 0, "ps": 0, "sx": 0}
+    seen = {}
+
+    def wait(q, sem, val):
+        if seen.get((q, sem), 0) < val:
+            seen[(q, sem)] = val
+            queue[q].wait_ge(T.sem[sem], val)
+
+    def done(sem, ins):
+        ins.then_inc(T.sem[sem], 1)
+        count[sem] += 1
+        return count[sem]
+
+    def V(ins):
+        return done("vs", ins)
+
+    def A(ins):
+        return done("acs", ins)
+
+    def vself():
+        wait("v", "vs", count["vs"])
+
+    g.sync.dma_start(T.LAND[:, 0, 0:LT], T.src[:]).then_inc(T.sem.ld, 16)
+    g.scalar.dma_start(T.LAND[:, 0, LT:2 * LT], T.dst[:]).then_inc(T.sem.ld, 16)
+    g.sync.dma_start(T.TW[:, 0:1024], T.tab[:, 0:1024]).then_inc(T.sem.tl, 16)
+
+    V(g.vector.memset(T.U[:], 1.0))
+    ones = V(g.vector.memset(T.U2[:], 1.0))
+    V(g.vector.memset(T.ME[:], 0.0))
+    V(g.vector.memset(T.RSTE[:], 1.0))
+    vself()
+    for b in range(N):
+        V(g.vector.memset(T.RSTE[:, b * CWE:b * CWE + 1], 0.0))
+    ones_sel = V(g.vector.memset(T.SEL[:], 1.0))
+    V(g.vector.memset(T.M[:], 0.0))
+    V(g.vector.memset(T.RST[:], 1.0))
+    vself()
+    for b in range(N):
+        V(g.vector.memset(T.RST[:, b * CW:b * CW + 1], 0.0))
+    wait("g", "vs", ones)
+    loose = {"allow_small_or_imprecise_dtypes": True}
+    done("gs", g.affine_select(T.U[:], T.U[:], [[1, 128]], op.is_gt, 0.0, 0, -1))
+    c_u = done("gs", g.affine_select(T.U2[:], T.U2[:], [[-1, 128]], op.is_ge, 0.0, 0, 1))
+
+    g.wait_ge(T.sem.ld, 32)
+    sent = arrive = 0
+    for group, mask in ((off, outside), (on, inside)):
+        g.remote_dma_fused([RemoteDMATransfer(dst_ids=[dst_id(topo, T.cores[d], core) for d in group],
+                                              dma_engine_mask=mask, remote_sem=T.sem.la, srcs=[T.LAND[:, 0, :]],
+                                              dsts=[T.LAND[:, place(d, me), :] for d in group])], local_sem=T.sem.sn)
+        sent += len(bits(mask))
+        arrive += len(group) * len(bits(mask))
+    c_cb = done("gs", g.iota(T.CB[:], [[-2 * Q, MS + 1]], 1, 0, **loose))
+    done("gs", g.iota(T.IOT[:], [[1, 128]], 0, 0, **loose))
+    c_a = done("gs", g.iota(T.C16[:], [[Q, MS + 1]], 0, 0, **loose))
+    wait("g", "vs", ones_sel)
+    c_sel = done("gs", g.affine_select(T.SEL[:], T.SEL[:], [[-Q, 8], [0, 8], [-1, Q]], op.is_equal, 0.0, 0, 1))
+    done("gs", g.iota(T.CB2[:], [[-256, MS + 1]], 1, 0, **loose))
+    done("gs", g.iota(T.C128[:], [[128, MS + 1]], 0, 0, **loose))
+    done("gs", g.iota(T.FH[:], [[Q, R // Q]], 0, 0, **loose))
+    c_f = done("gs", g.iota(T.FL[:], [[0, R // Q]], 0, 1, **loose))
+    g.sync.wait_ge(T.sem.sn, sent)
+    g.sync.dma_start(T.TW[:, 1024:R], T.tab[:, 1024:R]).then_inc(T.sem.tl, 16)
+
+    def classes(high, low, n, big):
+        V(g.vector.tensor_scalar(T.NM[:, 0:n], high[:, 0:n], float(me), big, op.not_equal, op.mult))
+        vself()
+        V(g.vector.tensor_tensor(T.X[:, 0:n], low[:, 0:n], T.NM[:, 0:n], op.add))
+        vself()
+
+    def counts(m, cw, base):
+        wait("p", "gs", c_u)
+        wait("p", "vs", count["vs"])
+        w = N * cw
+        g.tensor.matmul(T.PINC[:, 0:w - 1], T.U[:], m[:, 1:w], True, False)
+        if base:
+            g.tensor.matmul(T.PINC[:, 0:w - 1], T.ONE[0:1, :], T.BASE[0:1, 0:w - 1], False, False)
+        return done("ps", g.tensor.matmul(T.PINC[:, 0:w - 1], T.U2[:], m[:, 0:w - 1], False, True))
+
+    def scan(rst, cw, mark):
+        wait("v", "ps", mark)
+        w = N * cw - 1
+        V(g.vector.tensor_tensor_scan(T.PZ[:, 0:w], rst[:, 0:w], T.PINC[:, 0:w], 0.0, op.mult, op.add))
+        vself()
+
+    def merge(cw):
+        vself()
+        h = 3 * cw
+        V(g.vector.tensor_tensor(T.R1[:, 0:h - 1], T.MZ[:, 0:h - 1], T.MZ[:, h:2 * h - 1], op.add))
+        vself()
+        V(g.vector.tensor_tensor(T.R2[:, 0:cw - 1], T.R1[:, 0:cw - 1], T.R1[:, cw:2 * cw - 1], op.add))
+        vself()
+
+    def last(out, cw):
+        return V(g.vector.tensor_tensor(out[:, 0:cw - 1], T.R2[:, 0:cw - 1], T.R1[:, 2 * cw:3 * cw - 1], op.add))
+
+    def source_keys(lists, m, rst, pos):
+        n = lists * LT
+        cw, w = n + 1, N * (n + 1)
+        S, D = T.LAND[:, 0:lists, 0:LT], T.LAND[:, 0:lists, LT:2 * LT]
+        V(g.vector.tensor_scalar(T.SH[:, 0:n], S, 12, None, op.arith_shift_right))
+        V(g.vector.tensor_scalar(T.DH[:, 0:n], D, 12, None, op.arith_shift_right))
+        vself()
+        classes(T.SH, T.DH, n, 64.0)
+        for b in range(N):
+            V(g.vector.tensor_scalar(m[:, b * cw + 1:b * cw + cw], T.X[:, 0:n], float(b), None, op.is_equal))
+        mark = counts(m, cw, False)
+        low = V(g.vector.tensor_scalar(T.LOW[:, 0:n], S, R - 1, None, op.bitwise_and))
+        V(g.vector.tensor_scalar(T.X16[:, 0:n], T.X[:, 0:n], float(Q), None, op.mult))
+        wait("v", "vs", low)
+        V(g.vector.tensor_scalar(T.VAL[:, 0:n], T.LOW[:, 0:n], -float(MID), None, op.add))
+        scan(rst, cw, mark)
+        V(g.vector.tensor_tensor(T.MZ[:, 0:w - 1], m[:, 1:w], T.PZ[:, 0:w - 1], op.mult))
+        merge(cw)
+        posi = last(T.POSI, cw)
+        wait("a", "vs", last(pos, cw))
+        wait("v", "vs", posi)
+        V(g.vector.tensor_scalar(T.REM[:, 0:n], T.POSI[:, 0:n], Q - 1, None, op.bitwise_and))
+        vself()
+        V(g.vector.tensor_tensor(T.KEY[:, 0:n], T.REM[:, 0:n], T.X16[:, 0:n], op.add))
+        vself()
+
+    def rows(t0, t1, a, w, b, cb, cv, at):
+        ready = []
+        for t in range(t0, t1):
+            if t % 5 == 4:
+                V(g.vector.tensor_scalar(b[:, t, 0:MS + 1], cv[:], at[:, t:t + 1], 2.0, op.is_le, op.mult))
+            else:
+                A(g.scalar.activation(b[:, t, 0:MS + 1], cb[:], fn.Sign, bias=at[:, t:t + 1], scale=0.5))
+            V(g.vector.tensor_scalar(a[:, t, :], T.IOT[:, 0:w], T.KEY[:, t:t + 1], T.VAL[:, t:t + 1],
+                                     op.is_equal, op.mult))
+            ready.append((count["vs"], count["acs"]))
+        return ready
+
+    def product(out, w, a, b, ready):
+        step = 4
+        for t in range(NT):
+            if t % step == 0:
+                v, s = ready[t + step - 1]
+                wait("p", "vs", v)
+                wait("p", "acs", s)
+            ins = g.tensor.matmul(out[0:w, 0:MS + 1], a[:, t, :], b[:, t, 0:MS + 1], t == 0, t == NT - 1)
+        return done("ps", ins)
+
+    def differences(out, w, mark):
+        wait("v", "ps", mark)
+        V(g.vector.tensor_copy(T.OC[0:w, :], out[0:w, 0:MS]))
+        vself()
+        V(g.vector.tensor_tensor(T.DIF[0:w, :], T.OC[0:w, :], out[0:w, 1:MS + 1], op.subtract))
+        wait("p", "vs", count["vs"])
+
+    w1 = N * Q
+    g.vector.wait_ge(T.sem.ld, 32)
+    source_keys(1, T.ME, T.RSTE, T.POSE)
+    wait("v", "gs", c_a)
+    wait("a", "gs", c_cb)
+    ready = rows(0, LT, T.A1, w1, T.B1, T.CB, T.C16, T.POSE)
+    g.vector.wait_ge(T.sem.la, arrive)
+    source_keys(N, T.M, T.RST, T.POS)
+    ready += rows(LT, NT, T.A1, w1, T.B1, T.CB, T.C16, T.POS)
+    mark = product(T.PO, w1, T.A1, T.B1, ready)
+    V(g.vector.memset(T.ONE[:], 1.0))
+    V(g.vector.memset(T.NZ[:], -0.0))
+    V(g.vector.memset(T.M2[:], 0.0))
+    differences(T.PO, w1, mark)
+    wait("p", "gs", c_sel)
+    near = sorted(on + [me])
+    marks = {}
+    for ps, bs in ((T.PWO, off), (T.PWN, near)):
+        for i, b in enumerate(bs):
+            marks[bs[0]] = done("ps", g.tensor.matmul(ps[:, i * MS:(i + 1) * MS], T.SEL[0:w1, b * 128:(b + 1) * 128],
+                                                      T.DIF[0:w1, :], True, True))
+    ofs = {}
+    for ps, bs in ((T.PWO, off), (T.PWN, near)):
+        wait("v", "ps", marks[bs[0]])
+        ofs[bs[0]] = V(g.vector.tensor_scalar(T.OFS[:, bs[0] * MS:(bs[-1] + 1) * MS], ps[:, 0:len(bs) * MS],
+                                              0.5, float(MID), op.mult, op.add))
+
+    def pick(eng, out, win):
+        if eng == "v":
+            V(g.vector.tensor_copy(out, win))
+        else:
+            A(g.scalar.activation(out, win, fn.Identity, bias=T.NZ[:, 0:1]))
+        return count["vs"], count["acs"]
+
+    to = landed(me)
+
+    def gather(eng, b, s0, s1):
+        out = T.TW[:, to + s0:to + s1] if b == me else T.SEND[:, b, s0:s1]
+        return pick(eng, out, T.TW[:, 0:R].indirect(T.OFS[:, b * MS + s0 // Q:b * MS + s1 // Q]))
+
+    for q in ("v", "a"):
+        wait(q, "vs", ofs[off[0]])
+        wait(q, "tl", 32)
+    got = {}
+    for s0, s1 in ((0, PR), (PR, CAPP)):
+        for i, b in enumerate(off):
+            got[(b, s0)] = gather("v" if i < len(off) // 2 else "a", b, s0, s1)
+    wait("a", "vs", ofs[near[0]])
+    for b in on + [me]:
+        got[b] = gather("a", b, 0, CAPP)
+
+    def send(marks, items, mask):
+        wait("g", "vs", max(m[0] for m in marks))
+        wait("g", "acs", max(m[1] for m in marks))
+        ms, k = split(mask, len(items))
+        g.remote_dma_fused([RemoteDMATransfer(dst_ids=[dst_id(topo, c, core)], dma_engine_mask=m, remote_sem=T.sem[s],
+                                              src=a, dst=b) for m, (c, s, a, b) in zip(ms, items)], local_sem=T.sem.sx)
+        count["sx"] += k * len(items)
+
+    mine = relays(T, topo, me)
+    for j in range(len(mine[0][1])):
+        send([got[(d[j], 0)] for _, d in mine],
+             [(c, "rl%d" % j, T.SEND[:, d[j], 0:PR], T.RB[:, j, :]) for c, d in mine], inside)
+        if j == 0:
+            send([got[(b, PR)] for b in off],
+                 [(T.cores[b], "rb%d" % me, T.SEND[:, b, PR:CAPP], T.TW[:, to + PR:to + CAPP]) for b in off], outside)
+    for now in portions(on):
+        send([got[b] for b in now],
+             [(T.cores[b], "rc%d" % me, T.SEND[:, b, :], T.TW[:, to:to + CAPP]) for b in now], inside)
+
+    V(g.vector.memset(T.BASE[:], 0.0))
+    V(g.vector.memset(T.TW[:, R + MID:R + MID + GAP], 0.0))
+    vself()
+    for b in range(N):
+        V(g.vector.memset(T.BASE[:, b * CW:b * CW + 1], float(landed(b) - R - MID)))
+    D = T.LAND[:, :, LT:2 * LT]
+    classes(T.DH, T.SH, NT, 256.0)
+    for a in range(N):
+        for i, j, n in runs(me, a):
+            c = a * CW + i * LT
+            V(g.vector.tensor_scalar(T.M2[:, c + 1:c + 1 + n * LT], T.X[:, j * LT:(j + n) * LT], float(a), None,
+                                     op.is_equal))
+    mark = counts(T.M2, CW, True)
+    low = V(g.vector.tensor_scalar(T.LOW[:], D, R - 1, None, op.bitwise_and))
+    rem = V(g.vector.tensor_scalar(T.REM[:], D, 127, None, op.bitwise_and))
+    wait("v", "vs", low)
+    dlf = V(g.vector.tensor_copy(T.DLF[:], T.LOW[:]))
+    wait("v", "vs", rem)
+    V(g.vector.tensor_tensor(T.KEY[:], T.REM[:], T.NM[:], op.add))
+    scan(T.RST, CW, mark)
+    for a in range(N):
+        for i, j, n in runs(me, a):
+            c = a * CW + i * LT
+            V(g.vector.tensor_tensor(T.MZ[:, a * CW + j * LT:a * CW + (j + n) * LT], T.M2[:, c + 1:c + 1 + n * LT],
+                                     T.PZ[:, c:c + n * LT], op.mult))
+    merge(CW)
+    last(T.VAL, CW)
+    vself()
+    wait("p", "gs", c_f)
+    wait("p", "vs", count["vs"])
+    c = R // Q
+    g.tensor.matmul(T.PW2[:, 0:c], T.SEL[0:Q, 0:128], T.FH[0:Q, :], True, False)
+    mark = done("ps", g.tensor.matmul(T.PW2[:, 0:c], T.SEL[0:Q, 0:128], T.FL[0:Q, :], False, True))
+    wait("v", "gs", c_f)
+    wait("a", "gs", c_f)
+    wait("a", "vs", dlf)
+    ready = rows(0, NT, T.A2, 128, T.B2, T.CB2, T.C128, T.DLF)
+    wait("v", "ps", mark)
+    V(g.vector.tensor_scalar(T.KD[:], T.PW2[:, 0:c], -float(R + MID), 2.0, op.add, op.mult))
+    mark = product(T.PO2, 128, T.A2, T.B2, ready)
+    differences(T.PO2, 128, mark)
+    for r in range(8):
+        mark = done("ps", g.tensor.matmul(T.PW2[:, r:c:8], T.SEL[:, r * 128:(r + 1) * 128], T.DIF[:], True, True))
+    wait("v", "ps", mark)
+    V(g.vector.tensor_scalar(T.ADD[:], T.PW2[:, 0:c], 0.0, None, op.is_equal))
+    vself()
+    V(g.vector.tensor_tensor(T.ADD[:], T.ADD[:], T.KD[:], op.mult))
+    vself()
+    V(g.vector.tensor_tensor(T.ADD[:], T.ADD[:], T.PW2[:, 0:c], op.add))
+    vself()
+    inv = V(g.vector.tensor_scalar(T.INV[:], T.ADD[:], 0.5, float(R + MID), op.mult, op.add))
+
+    arrivals = []
+    for a in on:
+        o = others(T, topo, a)
+        inside_a = topo.mask(T.cores[a], core) & ~topo.mask(T.cores[a], T.cores[o[0][0]])
+        run = [p for p in portions(o[1]) if me in p][0]
+        arrivals.append(("rc%d" % a, split(inside_a, len(run))[1]))
+    for a in off:
+        arrivals.append(("rb%d" % a, split(topo.mask(T.cores[a], core), len(others(T, topo, a)[0]))[1]))
+        for c, dests in relays(T, topo, a):
+            if me in dests:
+                arrivals.append(("ra%d" % a, split(topo.mask(c, core), len(dests))[1]))
+    wait("v", "acs", count["acs"])
+    wait("a", "vs", inv)
+    wait("a", "acs", count["acs"])
+    vself()
+    for q in ("v", "a"):
+        for s, k in arrivals:
+            wait(q, s, k)
+    c = 0
+    for i, n in enumerate(YBLOCKS):
+        v, s = pick("va"[i % 2], T.YB[:, c:c + n], T.TW[:, 0:WIN].indirect(T.INV[:, c // Q:(c + n) // Q]))
+        if i % 2:
+            wait("s", "acs", s)
+        else:
+            wait("s", "vs", v)
+        g.sync.dma_start(T.y[:, c:c + n], T.YB[:, c:c + n]).then_inc(T.sem.st, 16)
+        c += n
+    g.wait_ge(T.sem.sx, count["sx"])
+    g.sync.wait_ge(T.sem.gs, count["gs"])
+    g.sync.wait_ge(T.sem.ps, count["ps"])
+    g.sync.wait_ge(T.sem.st, 16 * len(YBLOCKS))

@@ -11,11 +11,12 @@ CWE = LT + 1
 MWE = N * CWE
 Q = 16
 MS = CAPP // Q
-PR = 192
+PR = 224
 MID = R // 2
 GAP = 4
 WIN = R + N * CAPP + GAP
-YBLOCKS = [512, 1024, 1024, 1024, 512]
+FIRST = 1024
+YBLOCKS = [384, 1024, 1280, 1408]
 
 
 def sbuf(dtype, *shape):
@@ -34,18 +35,18 @@ SCRATCH = {
     "POSE": sbuf("float32", LT), "POS": sbuf("float32", NT), "DLF": sbuf("float32", NT),
     "IOT": sbuf("bfloat16", 128), "CB": sbuf("float32", MS + 1), "CB2": sbuf("float32", MS + 1),
     "C16": sbuf("bfloat16", MS + 1), "C128": sbuf("bfloat16", MS + 1),
-    "FH": sbuf("bfloat16", R // Q), "FL": sbuf("bfloat16", R // Q), "KD": sbuf("float32", R // Q),
+    "FH": sbuf("bfloat16", R // Q), "FL": sbuf("bfloat16", R // Q), "FC": sbuf("bfloat16", R // Q),
     "NZ": sbuf("float32", 1),
     "A1": sbuf("float16", NT, N * Q), "A2": sbuf("float16", NT, 128),
     "B1": sbuf("bfloat16", NT, MS + 2), "B2": sbuf("bfloat16", NT, MS + 2),
     "OC": sbuf("float32", MS), "DIF": sbuf("float16", MS), "ADD": sbuf("float32", R // Q),
     "OFS": sbuf("uint16", N * MS), "INV": sbuf("uint16", R // Q),
-    "TW": sbuf("float32", WIN), "SEND": sbuf("float32", N, CAPP), "YB": sbuf("float32", R),
-    "RB": sbuf("float32", 2, PR),
+    "TW": sbuf("float32", WIN), "YB": sbuf("float32", R),
+    "SREL": sbuf("float32", N, PR), "SEND": sbuf("float32", N, CAPP), "RB": sbuf("float32", 2, PR),
 }
-for _k in ("PINC", "PZ", "PO", "PWO", "PWN", "PO2", "PW2"):
+for _k in ("PINC", "PZ", "PO", "PWO", "PWN", "PO2", "PW2", "PKD"):
     SCRATCH[_k] = ("psum", [128, 512], "float32")
-SEMAPHORES = (["ld", "tl", "la", "sn", "sx", "st", "gs", "vs", "acs", "ps", "rl0", "rl1"]
+SEMAPHORES = (["ld", "go", "tl", "la", "sn", "sx", "st", "gs", "vs", "acs", "ps", "cs", "rl0", "rl1"]
               + ["r%s%d" % (p, a) for p in "abc" for a in range(N)])
 
 
@@ -70,6 +71,11 @@ def relays(T, topo, rank):
     mine = cand[i * k:(i + 1) * k]
     m = len(off) // k
     return [(mine[j], off[j * m:(j + 1) * m]) for j in range(k)]
+
+
+def turns(T, topo, rank):
+    r = relays(T, topo, rank)
+    return r if len(r) > 1 else [(c, [d]) for c, ds in r for d in ds]
 
 
 def bits(mask):
@@ -115,21 +121,37 @@ def dst_id(topo, dst, src):
 
 def relay_program(g, core, T, topo):
     for rank in range(N):
-        for c, dests in relays(T, topo, rank):
+        mine = relays(T, topo, rank)
+        for i, (c, dests) in enumerate(mine):
             if c != core:
                 continue
             src = T.cores[rank]
             off, _ = others(T, topo, rank)
             inside = topo.mask(src, core) & ~topo.mask(src, T.cores[off[0]])
-            _, k = split(inside, len(relays(T, topo, rank)))
-            masks, kk = split(topo.mask(core, T.cores[dests[0]]), len(dests))
+            outside = topo.mask(core, T.cores[dests[0]])
+            masks, k = split(outside, len(dests))
+            n = 8 // len(mine)
+            part = T.SEL[:, i * n * 128:(i + 1) * n * 128]
+            g.vector.memset(part, 0.5).then_inc(T.sem.vs, 1)
+            g.wait_ge(T.sem.vs, 1)
+            g.affine_select(part, part, [[-Q, n], [0, 8], [-1, Q]], AluOpType.is_equal, 0.0, -Q * i * n,
+                            1).then_inc(T.sem.gs, 1)
+            g.wait_ge(T.sem.gs, 1)
+            g.remote_dma_fused([RemoteDMATransfer(dst_ids=[dst_id(topo, src, core)], dma_engine_mask=outside,
+                                                  remote_sem=T.sem.cs, src=part, dst=part)], local_sem=T.sem.sx)
             to = landed(rank)
-            for j, d in enumerate(dests):
-                g.wait_ge(T.sem["rl%d" % j], k)
-                g.remote_dma_fused([RemoteDMATransfer(dst_ids=[dst_id(topo, T.cores[d], core)], dma_engine_mask=masks[j],
-                                                      remote_sem=T.sem["ra%d" % rank], src=T.RB[:, j, :],
-                                                      dst=T.TW[:, to:to + PR])], local_sem=T.sem.sx)
-            g.wait_ge(T.sem.sx, kk * len(dests))
+            for j, (relay, now) in enumerate(turns(T, topo, rank)):
+                if relay != core:
+                    continue
+                g.wait_ge(T.sem["rl%d" % j], len(bits(inside)))
+                tr = []
+                for d in now:
+                    e = dests.index(d)
+                    tr.append(RemoteDMATransfer(dst_ids=[dst_id(topo, T.cores[d], core)], dma_engine_mask=masks[e],
+                                                remote_sem=T.sem["ra%d" % rank], src=T.RB[:, e, :],
+                                                dst=T.TW[:, to:to + PR]))
+                g.remote_dma_fused(tr, local_sem=T.sem.sx)
+            g.wait_ge(T.sem.sx, k * len(dests) + len(bits(outside)))
 
 
 def rank_program(g, core, T, topo):
@@ -140,6 +162,7 @@ def rank_program(g, core, T, topo):
     off, on = others(T, topo, me)
     outside = topo.mask(core, T.cores[off[0]])
     inside = topo.mask(core, T.cores[on[0]]) & ~outside
+    mine = relays(T, topo, me)
     queue = {"g": g, "v": g.vector, "a": g.scalar, "p": g.tensor, "s": g.sync}
     count = {"gs": 0, "vs": 0, "acs": 0, "ps": 0, "sx": 0}
     seen = {}
@@ -165,7 +188,7 @@ def rank_program(g, core, T, topo):
 
     g.sync.dma_start(T.LAND[:, 0, 0:LT], T.src[:]).then_inc(T.sem.ld, 16)
     g.scalar.dma_start(T.LAND[:, 0, LT:2 * LT], T.dst[:]).then_inc(T.sem.ld, 16)
-    g.sync.dma_start(T.TW[:, 0:1024], T.tab[:, 0:1024]).then_inc(T.sem.tl, 16)
+    g.sync.dma_start(T.TW[:, 0:FIRST], T.tab[:, 0:FIRST]).then_inc(T.sem.tl, 16)
 
     V(g.vector.memset(T.U[:], 1.0))
     ones = V(g.vector.memset(T.U2[:], 1.0))
@@ -174,7 +197,6 @@ def rank_program(g, core, T, topo):
     vself()
     for b in range(N):
         V(g.vector.memset(T.RSTE[:, b * CWE:b * CWE + 1], 0.0))
-    ones_sel = V(g.vector.memset(T.SEL[:], 1.0))
     V(g.vector.memset(T.M[:], 0.0))
     V(g.vector.memset(T.RST[:], 1.0))
     vself()
@@ -193,43 +215,38 @@ def rank_program(g, core, T, topo):
                                               dsts=[T.LAND[:, place(d, me), :] for d in group])], local_sem=T.sem.sn)
         sent += len(bits(mask))
         arrive += len(group) * len(bits(mask))
+    g.sem_inc(T.sem.go, 1)
+    g.sync.wait_ge(T.sem.go, 1)
+    g.sync.dma_start(T.TW[:, FIRST:R], T.tab[:, FIRST:R]).then_inc(T.sem.tl, 16)
     c_cb = done("gs", g.iota(T.CB[:], [[-2 * Q, MS + 1]], 1, 0, **loose))
     done("gs", g.iota(T.IOT[:], [[1, 128]], 0, 0, **loose))
     c_a = done("gs", g.iota(T.C16[:], [[Q, MS + 1]], 0, 0, **loose))
-    wait("g", "vs", ones_sel)
-    c_sel = done("gs", g.affine_select(T.SEL[:], T.SEL[:], [[-Q, 8], [0, 8], [-1, Q]], op.is_equal, 0.0, 0, 1))
     done("gs", g.iota(T.CB2[:], [[-256, MS + 1]], 1, 0, **loose))
     done("gs", g.iota(T.C128[:], [[128, MS + 1]], 0, 0, **loose))
-    done("gs", g.iota(T.FH[:], [[Q, R // Q]], 0, 0, **loose))
-    c_f = done("gs", g.iota(T.FL[:], [[0, R // Q]], 0, 1, **loose))
-    g.sync.wait_ge(T.sem.sn, sent)
-    g.sync.dma_start(T.TW[:, 1024:R], T.tab[:, 1024:R]).then_inc(T.sem.tl, 16)
+    done("gs", g.iota(T.FH[:], [[2 * Q, R // Q]], 0, 0, **loose))
+    c_f = done("gs", g.iota(T.FL[:], [[0, R // Q]], 0, 2, **loose))
 
-    def classes(high, low, n, big):
-        V(g.vector.tensor_scalar(T.NM[:, 0:n], high[:, 0:n], float(me), big, op.not_equal, op.mult))
-        vself()
-        V(g.vector.tensor_tensor(T.X[:, 0:n], low[:, 0:n], T.NM[:, 0:n], op.add))
-        vself()
-
-    def counts(m, cw, base):
+    def counts(bank, m, lo, hi, base):
         wait("p", "gs", c_u)
         wait("p", "vs", count["vs"])
-        w = N * cw
-        g.tensor.matmul(T.PINC[:, 0:w - 1], T.U[:], m[:, 1:w], True, False)
+        out = bank[:, 0:hi - lo]
+        g.tensor.matmul(out, T.U[:], m[:, lo + 1:hi + 1], True, False)
         if base:
-            g.tensor.matmul(T.PINC[:, 0:w - 1], T.ONE[0:1, :], T.BASE[0:1, 0:w - 1], False, False)
-        return done("ps", g.tensor.matmul(T.PINC[:, 0:w - 1], T.U2[:], m[:, 0:w - 1], False, True))
+            g.tensor.matmul(out, T.ONE[0:1, :], T.BASE[0:1, lo:hi], False, False)
+        return done("ps", g.tensor.matmul(out, T.U2[:], m[:, lo:hi], False, True))
 
-    def scan(rst, cw, mark):
-        wait("v", "ps", mark)
-        w = N * cw - 1
-        V(g.vector.tensor_tensor_scan(T.PZ[:, 0:w], rst[:, 0:w], T.PINC[:, 0:w], 0.0, op.mult, op.add))
-        vself()
+    def scans(rst, h, w, marks):
+        wait("v", "ps", marks[0])
+        V(g.vector.tensor_tensor_scan(T.PZ[:, 0:h], rst[:, 0:h], T.PINC[:, 0:h], 0.0, op.mult, op.add))
+        first = count["vs"]
+        wait("v", "ps", marks[1])
+        V(g.vector.tensor_tensor_scan(T.PZ[:, h:w], rst[:, h:w], T.PO2[:, 0:w - h], 0.0, op.mult, op.add))
+        wait("v", "vs", first)
 
     def merge(cw):
+        w = 3 * cw - 1
         vself()
-        h = 3 * cw
-        V(g.vector.tensor_tensor(T.R1[:, 0:h - 1], T.MZ[:, 0:h - 1], T.MZ[:, h:2 * h - 1], op.add))
+        V(g.vector.tensor_tensor(T.R1[:, 0:w], T.MZ[:, 0:w], T.PW2[:, 0:w], op.add))
         vself()
         V(g.vector.tensor_tensor(T.R2[:, 0:cw - 1], T.R1[:, 0:cw - 1], T.R1[:, cw:2 * cw - 1], op.add))
         vself()
@@ -239,21 +256,30 @@ def rank_program(g, core, T, topo):
 
     def source_keys(lists, m, rst, pos):
         n = lists * LT
-        cw, w = n + 1, N * (n + 1)
+        cw = n + 1
+        h, w = 3 * cw, 6 * cw - 1
         S, D = T.LAND[:, 0:lists, 0:LT], T.LAND[:, 0:lists, LT:2 * LT]
         V(g.vector.tensor_scalar(T.SH[:, 0:n], S, 12, None, op.arith_shift_right))
         V(g.vector.tensor_scalar(T.DH[:, 0:n], D, 12, None, op.arith_shift_right))
         vself()
-        classes(T.SH, T.DH, n, 64.0)
-        for b in range(N):
-            V(g.vector.tensor_scalar(m[:, b * cw + 1:b * cw + cw], T.X[:, 0:n], float(b), None, op.is_equal))
-        mark = counts(m, cw, False)
+        V(g.vector.tensor_scalar(T.NM[:, 0:n], T.SH[:, 0:n], float(me), 64.0, op.not_equal, op.mult))
+        vself()
+        V(g.vector.tensor_tensor(T.X[:, 0:n], T.DH[:, 0:n], T.NM[:, 0:n], op.add))
+        vself()
+        marks = []
+        for bank, b0, lo, hi in ((T.PINC, 0, 0, h), (T.PO2, 3, h, w)):
+            for b in range(b0, b0 + 3):
+                V(g.vector.tensor_scalar(m[:, b * cw + 1:b * cw + cw], T.X[:, 0:n], float(b), None, op.is_equal))
+            marks.append(counts(bank, m, lo, hi, False))
         low = V(g.vector.tensor_scalar(T.LOW[:, 0:n], S, R - 1, None, op.bitwise_and))
         V(g.vector.tensor_scalar(T.X16[:, 0:n], T.X[:, 0:n], float(Q), None, op.mult))
         wait("v", "vs", low)
         V(g.vector.tensor_scalar(T.VAL[:, 0:n], T.LOW[:, 0:n], -float(MID), None, op.add))
-        scan(rst, cw, mark)
-        V(g.vector.tensor_tensor(T.MZ[:, 0:w - 1], m[:, 1:w], T.PZ[:, 0:w - 1], op.mult))
+        scans(rst, h, w, marks)
+        second = count["vs"]
+        V(g.vector.tensor_tensor(T.MZ[:, 0:h - 1], m[:, 1:h], T.PZ[:, 0:h - 1], op.mult))
+        wait("v", "vs", second)
+        V(g.vector.tensor_tensor(T.PW2[:, 0:h - 1], m[:, h + 1:w + 1], T.PZ[:, h:w], op.mult))
         merge(cw)
         posi = last(T.POSI, cw)
         wait("a", "vs", last(pos, cw))
@@ -263,10 +289,10 @@ def rank_program(g, core, T, topo):
         V(g.vector.tensor_tensor(T.KEY[:, 0:n], T.REM[:, 0:n], T.X16[:, 0:n], op.add))
         vself()
 
-    def rows(t0, t1, a, w, b, cb, cv, at):
+    def rows(t0, t1, a, w, b, cb, cv, at, share):
         ready = []
         for t in range(t0, t1):
-            if t % 5 == 4:
+            if t % share == 1:
                 V(g.vector.tensor_scalar(b[:, t, 0:MS + 1], cv[:], at[:, t:t + 1], 2.0, op.is_le, op.mult))
             else:
                 A(g.scalar.activation(b[:, t, 0:MS + 1], cb[:], fn.Sign, bias=at[:, t:t + 1], scale=0.5))
@@ -278,6 +304,8 @@ def rank_program(g, core, T, topo):
     def product(out, w, a, b, ready):
         step = 4
         for t in range(NT):
+            if t == NT - step:
+                step = 2
             if t % step == 0:
                 v, s = ready[t + step - 1]
                 wait("p", "vs", v)
@@ -295,18 +323,32 @@ def rank_program(g, core, T, topo):
     w1 = N * Q
     g.vector.wait_ge(T.sem.ld, 32)
     source_keys(1, T.ME, T.RSTE, T.POSE)
-    wait("v", "gs", c_a)
-    wait("a", "gs", c_cb)
-    ready = rows(0, LT, T.A1, w1, T.B1, T.CB, T.C16, T.POSE)
-    g.vector.wait_ge(T.sem.la, arrive)
-    source_keys(N, T.M, T.RST, T.POS)
-    ready += rows(LT, NT, T.A1, w1, T.B1, T.CB, T.C16, T.POS)
-    mark = product(T.PO, w1, T.A1, T.B1, ready)
     V(g.vector.memset(T.ONE[:], 1.0))
     V(g.vector.memset(T.NZ[:], -0.0))
     V(g.vector.memset(T.M2[:], 0.0))
+    V(g.vector.memset(T.BASE[:], 0.0))
+    V(g.vector.memset(T.FC[:], -float(R + MID)))
+    V(g.vector.memset(T.TW[:, R + MID:R + MID + GAP], 0.0))
+    vself()
+    for b in range(N):
+        V(g.vector.memset(T.BASE[:, b * CW:b * CW + 1], float(landed(b) - R - MID)))
+    wait("v", "gs", c_a)
+    wait("a", "gs", c_cb)
+    ready = rows(0, LT, T.A1, w1, T.B1, T.CB, T.C16, T.POSE, 5)
+    g.vector.wait_ge(T.sem.la, arrive)
+    source_keys(N, T.M, T.RST, T.POS)
+    ready += rows(LT, NT, T.A1, w1, T.B1, T.CB, T.C16, T.POS, 5)
+    mark = product(T.PO, w1, T.A1, T.B1, ready)
+    D = T.LAND[:, :, LT:2 * LT]
+    nm = V(g.vector.tensor_scalar(T.NM[:], T.DH[:], float(me), 256.0, op.not_equal, op.mult))
+    V(g.vector.tensor_scalar(T.LOW[:], D, R - 1, None, op.bitwise_and))
+    V(g.vector.tensor_scalar(T.REM[:], D, 127, None, op.bitwise_and))
+    wait("v", "vs", nm)
+    V(g.vector.tensor_tensor(T.X[:], T.SH[:], T.NM[:], op.add))
     differences(T.PO, w1, mark)
-    wait("p", "gs", c_sel)
+    dlf = V(g.vector.tensor_copy(T.DLF[:], T.LOW[:]))
+    V(g.vector.tensor_tensor(T.KEY[:], T.REM[:], T.NM[:], op.add))
+    g.tensor.wait_ge(T.sem.cs, len(mine) * len(bits(outside)))
     near = sorted(on + [me])
     marks = {}
     for ps, bs in ((T.PWO, off), (T.PWN, near)):
@@ -317,7 +359,11 @@ def rank_program(g, core, T, topo):
     for ps, bs in ((T.PWO, off), (T.PWN, near)):
         wait("v", "ps", marks[bs[0]])
         ofs[bs[0]] = V(g.vector.tensor_scalar(T.OFS[:, bs[0] * MS:(bs[-1] + 1) * MS], ps[:, 0:len(bs) * MS],
-                                              0.5, float(MID), op.mult, op.add))
+                                              float(MID), None, op.add))
+    wait("p", "gs", c_f)
+    g.tensor.matmul(T.PKD[:, 0:R // Q], T.SEL[0:Q, 0:128], T.FH[0:Q, :], True, False)
+    g.tensor.matmul(T.PKD[:, 0:R // Q], T.ONE[0:1, :], T.FC[0:1, :], False, False)
+    pkd = done("ps", g.tensor.matmul(T.PKD[:, 0:R // Q], T.SEL[0:Q, 0:128], T.FL[0:Q, :], False, True))
 
     def pick(eng, out, win):
         if eng == "v":
@@ -329,16 +375,22 @@ def rank_program(g, core, T, topo):
     to = landed(me)
 
     def gather(eng, b, s0, s1):
-        out = T.TW[:, to + s0:to + s1] if b == me else T.SEND[:, b, s0:s1]
+        if b == me:
+            out = T.TW[:, to + s0:to + s1]
+        elif s1 == PR:
+            out = T.SREL[:, off.index(b), :]
+        else:
+            out = T.SEND[:, b, s0:s1]
         return pick(eng, out, T.TW[:, 0:R].indirect(T.OFS[:, b * MS + s0 // Q:b * MS + s1 // Q]))
 
     for q in ("v", "a"):
         wait(q, "vs", ofs[off[0]])
         wait(q, "tl", 32)
     got = {}
-    for s0, s1 in ((0, PR), (PR, CAPP)):
-        for i, b in enumerate(off):
-            got[(b, s0)] = gather("v" if i < len(off) // 2 else "a", b, s0, s1)
+    feed = turns(T, topo, me)
+    for bs, s0, s1 in ((feed[0][1], 0, PR), (off, PR, CAPP), (feed[1][1], 0, PR)):
+        for b in bs:
+            got[(b, s0)] = gather("va"[off.index(b) % 2], b, s0, s1)
     wait("a", "vs", ofs[near[0]])
     for b in on + [me]:
         got[b] = gather("a", b, 0, CAPP)
@@ -351,10 +403,9 @@ def rank_program(g, core, T, topo):
                                               src=a, dst=b) for m, (c, s, a, b) in zip(ms, items)], local_sem=T.sem.sx)
         count["sx"] += k * len(items)
 
-    mine = relays(T, topo, me)
-    for j in range(len(mine[0][1])):
-        send([got[(d[j], 0)] for _, d in mine],
-             [(c, "rl%d" % j, T.SEND[:, d[j], 0:PR], T.RB[:, j, :]) for c, d in mine], inside)
+    for j, (c, now) in enumerate(feed):
+        i, e, n = off.index(now[0]), dict(mine)[c].index(now[0]), len(now)
+        send([got[(b, 0)] for b in now], [(c, "rl%d" % j, T.SREL[:, i:i + n, :], T.RB[:, e:e + n, :])], inside)
         if j == 0:
             send([got[(b, PR)] for b in off],
                  [(T.cores[b], "rb%d" % me, T.SEND[:, b, PR:CAPP], T.TW[:, to + PR:to + CAPP]) for b in off], outside)
@@ -362,57 +413,43 @@ def rank_program(g, core, T, topo):
         send([got[b] for b in now],
              [(T.cores[b], "rc%d" % me, T.SEND[:, b, :], T.TW[:, to:to + CAPP]) for b in now], inside)
 
-    V(g.vector.memset(T.BASE[:], 0.0))
-    V(g.vector.memset(T.TW[:, R + MID:R + MID + GAP], 0.0))
+    h, w = 3 * CW, MW - 1
     vself()
-    for b in range(N):
-        V(g.vector.memset(T.BASE[:, b * CW:b * CW + 1], float(landed(b) - R - MID)))
-    D = T.LAND[:, :, LT:2 * LT]
-    classes(T.DH, T.SH, NT, 256.0)
-    for a in range(N):
-        for i, j, n in runs(me, a):
-            c = a * CW + i * LT
-            V(g.vector.tensor_scalar(T.M2[:, c + 1:c + 1 + n * LT], T.X[:, j * LT:(j + n) * LT], float(a), None,
-                                     op.is_equal))
-    mark = counts(T.M2, CW, True)
-    low = V(g.vector.tensor_scalar(T.LOW[:], D, R - 1, None, op.bitwise_and))
-    rem = V(g.vector.tensor_scalar(T.REM[:], D, 127, None, op.bitwise_and))
-    wait("v", "vs", low)
-    dlf = V(g.vector.tensor_copy(T.DLF[:], T.LOW[:]))
-    wait("v", "vs", rem)
-    V(g.vector.tensor_tensor(T.KEY[:], T.REM[:], T.NM[:], op.add))
-    scan(T.RST, CW, mark)
-    for a in range(N):
-        for i, j, n in runs(me, a):
-            c = a * CW + i * LT
-            V(g.vector.tensor_tensor(T.MZ[:, a * CW + j * LT:a * CW + (j + n) * LT], T.M2[:, c + 1:c + 1 + n * LT],
-                                     T.PZ[:, c:c + n * LT], op.mult))
+    marks = []
+    for bank, a0, lo, hi in ((T.PINC, 0, 0, h), (T.PO2, 3, h, w)):
+        for a in range(a0, a0 + 3):
+            for i, j, n in runs(me, a):
+                c = a * CW + 1 + i * LT
+                V(g.vector.tensor_scalar(T.M2[:, c:c + n * LT], T.X[:, j * LT:(j + n) * LT], float(a), None, op.is_equal))
+        marks.append(counts(bank, T.M2, lo, hi, True))
+    scans(T.RST, h, w, marks)
+    second = count["vs"]
+    for out, a0 in ((T.MZ, 0), (T.PW2, 3)):
+        for a in range(a0, a0 + 3):
+            for i, j, n in runs(me, a):
+                c, o = a * CW + i * LT, (a - a0) * CW + j * LT
+                V(g.vector.tensor_tensor(out[:, o:o + n * LT], T.M2[:, c + 1:c + 1 + n * LT], T.PZ[:, c:c + n * LT], op.mult))
+        wait("v", "vs", second)
     merge(CW)
     last(T.VAL, CW)
     vself()
-    wait("p", "gs", c_f)
-    wait("p", "vs", count["vs"])
-    c = R // Q
-    g.tensor.matmul(T.PW2[:, 0:c], T.SEL[0:Q, 0:128], T.FH[0:Q, :], True, False)
-    mark = done("ps", g.tensor.matmul(T.PW2[:, 0:c], T.SEL[0:Q, 0:128], T.FL[0:Q, :], False, True))
     wait("v", "gs", c_f)
     wait("a", "gs", c_f)
     wait("a", "vs", dlf)
-    ready = rows(0, NT, T.A2, 128, T.B2, T.CB2, T.C128, T.DLF)
-    wait("v", "ps", mark)
-    V(g.vector.tensor_scalar(T.KD[:], T.PW2[:, 0:c], -float(R + MID), 2.0, op.add, op.mult))
+    ready = rows(0, NT, T.A2, 128, T.B2, T.CB2, T.C128, T.DLF, 8)
     mark = product(T.PO2, 128, T.A2, T.B2, ready)
     differences(T.PO2, 128, mark)
+    c = R // Q
     for r in range(8):
         mark = done("ps", g.tensor.matmul(T.PW2[:, r:c:8], T.SEL[:, r * 128:(r + 1) * 128], T.DIF[:], True, True))
     wait("v", "ps", mark)
     V(g.vector.tensor_scalar(T.ADD[:], T.PW2[:, 0:c], 0.0, None, op.is_equal))
     vself()
-    V(g.vector.tensor_tensor(T.ADD[:], T.ADD[:], T.KD[:], op.mult))
+    V(g.vector.tensor_tensor(T.ADD[:], T.ADD[:], T.PKD[:, 0:c], op.mult))
     vself()
     V(g.vector.tensor_tensor(T.ADD[:], T.ADD[:], T.PW2[:, 0:c], op.add))
     vself()
-    inv = V(g.vector.tensor_scalar(T.INV[:], T.ADD[:], 0.5, float(R + MID), op.mult, op.add))
+    inv = V(g.vector.tensor_scalar(T.INV[:], T.ADD[:], float(R + MID), None, op.add))
 
     arrivals = []
     for a in on:
@@ -442,6 +479,7 @@ def rank_program(g, core, T, topo):
         g.sync.dma_start(T.y[:, c:c + n], T.YB[:, c:c + n]).then_inc(T.sem.st, 16)
         c += n
     g.wait_ge(T.sem.sx, count["sx"])
+    g.wait_ge(T.sem.sn, sent)
     g.sync.wait_ge(T.sem.gs, count["gs"])
     g.sync.wait_ge(T.sem.ps, count["ps"])
     g.sync.wait_ge(T.sem.st, 16 * len(YBLOCKS))

@@ -11,12 +11,15 @@ CWE = LT + 1
 MWE = N * CWE
 Q = 16
 MS = CAPP // Q
+BW = MS + 2
+BCH = -(-(NT - LT) // 3)
 PR = 224
+PAIR = 2
 MID = R // 2
 GAP = 4
 WIN = R + N * CAPP + GAP
 FIRST = 1024
-YBLOCKS = [384, 1024, 1280, 1408]
+YBLOCKS = [256, 512, 896, 1152, 1280]
 
 
 def sbuf(dtype, *shape):
@@ -27,18 +30,20 @@ SCRATCH = {
     "LAND": sbuf("int32", N, 2 * LT),
     "M": sbuf("bfloat16", MW), "RST": sbuf("float32", MW), "ME": sbuf("bfloat16", MWE), "RSTE": sbuf("float32", MWE),
     "M2": sbuf("bfloat16", MW), "BASE": sbuf("bfloat16", MW), "ONE": sbuf("bfloat16", 128),
-    "U": sbuf("bfloat16", 128), "U2": sbuf("bfloat16", 128), "SEL": sbuf("bfloat16", 8 * 128),
+    "U": sbuf("bfloat16", 129), "U2": sbuf("bfloat16", 128), "SEL": sbuf("bfloat16", 8 * 128),
+    "IDENT": sbuf("bfloat16", 128), "POSH": sbuf("float16", NT),
+    "EXP": sbuf("bfloat16", BCH * BW), "POST": sbuf("bfloat16", 3 * 128),
     "MZ": sbuf("float32", MW), "R1": sbuf("float32", 3 * CW), "R2": sbuf("float32", NT),
     "SH": sbuf("int32", NT), "DH": sbuf("int32", NT), "LOW": sbuf("int32", NT), "POSI": sbuf("int32", NT),
     "REM": sbuf("int32", NT), "NM": sbuf("float32", NT), "X": sbuf("float32", NT), "X16": sbuf("float32", NT),
     "KEY": sbuf("float32", NT), "VAL": sbuf("float32", NT),
-    "POSE": sbuf("float32", LT), "POS": sbuf("float32", NT), "DLF": sbuf("float32", NT),
+    "POSE": sbuf("float32", LT), "DLF": sbuf("float32", NT),
     "IOT": sbuf("bfloat16", 128), "CB": sbuf("float32", MS + 1), "CB2": sbuf("float32", MS + 1),
-    "C16": sbuf("bfloat16", MS + 1), "C128": sbuf("bfloat16", MS + 1),
+    "C128": sbuf("bfloat16", MS + 1),
     "FH": sbuf("bfloat16", R // Q), "FL": sbuf("bfloat16", R // Q), "FC": sbuf("bfloat16", R // Q),
     "NZ": sbuf("float32", 1),
     "A1": sbuf("float16", NT, N * Q), "A2": sbuf("float16", NT, 128),
-    "B1": sbuf("bfloat16", NT, MS + 2), "B2": sbuf("bfloat16", NT, MS + 2),
+    "B1": sbuf("bfloat16", NT * BW), "B2": sbuf("bfloat16", NT, MS + 2),
     "OC": sbuf("float32", MS), "DIF": sbuf("float16", MS), "ADD": sbuf("float32", R // Q),
     "OFS": sbuf("uint16", N * MS), "INV": sbuf("uint16", R // Q),
     "TW": sbuf("float32", WIN), "YB": sbuf("float32", R),
@@ -46,7 +51,7 @@ SCRATCH = {
 }
 for _k in ("PINC", "PZ", "PO", "PWO", "PWN", "PO2", "PW2", "PKD"):
     SCRATCH[_k] = ("psum", [128, 512], "float32")
-SEMAPHORES = (["ld", "go", "tl", "la", "sn", "sx", "st", "gs", "vs", "acs", "ps", "cs", "rl0", "rl1"]
+SEMAPHORES = (["ld", "go", "tl", "la", "sn", "sx", "st", "gs", "vs", "acs", "ps", "cs", "rl0", "rl1", "iv", "cu"]
               + ["r%s%d" % (p, a) for p in "abc" for a in range(N)])
 
 
@@ -71,6 +76,10 @@ def relays(T, topo, rank):
     mine = cand[i * k:(i + 1) * k]
     m = len(off) // k
     return [(mine[j], off[j * m:(j + 1) * m]) for j in range(k)]
+
+
+def helper_of(T, topo, rank):
+    return relays(T, topo, rank)[0][0]
 
 
 def turns(T, topo, rank):
@@ -101,6 +110,10 @@ def portions(items):
     return out
 
 
+def pairs_of(off):
+    return [off[i:i + PAIR] for i in range(0, len(off), PAIR)]
+
+
 def place(r, c):
     return (c - r) % N
 
@@ -119,50 +132,8 @@ def dst_id(topo, dst, src):
     return DstId(rid=rid, pnc=pid)
 
 
-def relay_program(g, core, T, topo):
-    for rank in range(N):
-        mine = relays(T, topo, rank)
-        for i, (c, dests) in enumerate(mine):
-            if c != core:
-                continue
-            src = T.cores[rank]
-            off, _ = others(T, topo, rank)
-            inside = topo.mask(src, core) & ~topo.mask(src, T.cores[off[0]])
-            outside = topo.mask(core, T.cores[dests[0]])
-            masks, k = split(outside, len(dests))
-            n = 8 // len(mine)
-            part = T.SEL[:, i * n * 128:(i + 1) * n * 128]
-            g.vector.memset(part, 0.5).then_inc(T.sem.vs, 1)
-            g.wait_ge(T.sem.vs, 1)
-            g.affine_select(part, part, [[-Q, n], [0, 8], [-1, Q]], AluOpType.is_equal, 0.0, -Q * i * n,
-                            1).then_inc(T.sem.gs, 1)
-            g.wait_ge(T.sem.gs, 1)
-            g.remote_dma_fused([RemoteDMATransfer(dst_ids=[dst_id(topo, src, core)], dma_engine_mask=outside,
-                                                  remote_sem=T.sem.cs, src=part, dst=part)], local_sem=T.sem.sx)
-            to = landed(rank)
-            for j, (relay, now) in enumerate(turns(T, topo, rank)):
-                if relay != core:
-                    continue
-                g.wait_ge(T.sem["rl%d" % j], len(bits(inside)))
-                tr = []
-                for d in now:
-                    e = dests.index(d)
-                    tr.append(RemoteDMATransfer(dst_ids=[dst_id(topo, T.cores[d], core)], dma_engine_mask=masks[e],
-                                                remote_sem=T.sem["ra%d" % rank], src=T.RB[:, e, :],
-                                                dst=T.TW[:, to:to + PR]))
-                g.remote_dma_fused(tr, local_sem=T.sem.sx)
-            g.wait_ge(T.sem.sx, k * len(dests) + len(bits(outside)))
-
-
-def rank_program(g, core, T, topo):
-    me = T.rank_of(core)
-    if me is None:
-        return relay_program(g, core, T, topo)
-    op, fn = AluOpType, ActivationFunctionType
-    off, on = others(T, topo, me)
-    outside = topo.mask(core, T.cores[off[0]])
-    inside = topo.mask(core, T.cores[on[0]]) & ~outside
-    mine = relays(T, topo, me)
+def tools(g, T):
+    op = AluOpType
     queue = {"g": g, "v": g.vector, "a": g.scalar, "p": g.tensor, "s": g.sync}
     count = {"gs": 0, "vs": 0, "acs": 0, "ps": 0, "sx": 0}
     seen = {}
@@ -186,51 +157,10 @@ def rank_program(g, core, T, topo):
     def vself():
         wait("v", "vs", count["vs"])
 
-    g.sync.dma_start(T.LAND[:, 0, 0:LT], T.src[:]).then_inc(T.sem.ld, 16)
-    g.scalar.dma_start(T.LAND[:, 0, LT:2 * LT], T.dst[:]).then_inc(T.sem.ld, 16)
-    g.sync.dma_start(T.TW[:, 0:FIRST], T.tab[:, 0:FIRST]).then_inc(T.sem.tl, 16)
-
-    V(g.vector.memset(T.U[:], 1.0))
-    ones = V(g.vector.memset(T.U2[:], 1.0))
-    V(g.vector.memset(T.ME[:], 0.0))
-    V(g.vector.memset(T.RSTE[:], 1.0))
-    vself()
-    for b in range(N):
-        V(g.vector.memset(T.RSTE[:, b * CWE:b * CWE + 1], 0.0))
-    V(g.vector.memset(T.M[:], 0.0))
-    V(g.vector.memset(T.RST[:], 1.0))
-    vself()
-    for b in range(N):
-        V(g.vector.memset(T.RST[:, b * CW:b * CW + 1], 0.0))
-    wait("g", "vs", ones)
-    loose = {"allow_small_or_imprecise_dtypes": True}
-    done("gs", g.affine_select(T.U[:], T.U[:], [[1, 128]], op.is_gt, 0.0, 0, -1))
-    c_u = done("gs", g.affine_select(T.U2[:], T.U2[:], [[-1, 128]], op.is_ge, 0.0, 0, 1))
-
-    g.wait_ge(T.sem.ld, 32)
-    sent = arrive = 0
-    for group, mask in ((off, outside), (on, inside)):
-        g.remote_dma_fused([RemoteDMATransfer(dst_ids=[dst_id(topo, T.cores[d], core) for d in group],
-                                              dma_engine_mask=mask, remote_sem=T.sem.la, srcs=[T.LAND[:, 0, :]],
-                                              dsts=[T.LAND[:, place(d, me), :] for d in group])], local_sem=T.sem.sn)
-        sent += len(bits(mask))
-        arrive += len(group) * len(bits(mask))
-    g.sem_inc(T.sem.go, 1)
-    g.sync.wait_ge(T.sem.go, 1)
-    g.sync.dma_start(T.TW[:, FIRST:R], T.tab[:, FIRST:R]).then_inc(T.sem.tl, 16)
-    c_cb = done("gs", g.iota(T.CB[:], [[-2 * Q, MS + 1]], 1, 0, **loose))
-    done("gs", g.iota(T.IOT[:], [[1, 128]], 0, 0, **loose))
-    c_a = done("gs", g.iota(T.C16[:], [[Q, MS + 1]], 0, 0, **loose))
-    done("gs", g.iota(T.CB2[:], [[-256, MS + 1]], 1, 0, **loose))
-    done("gs", g.iota(T.C128[:], [[128, MS + 1]], 0, 0, **loose))
-    done("gs", g.iota(T.FH[:], [[2 * Q, R // Q]], 0, 0, **loose))
-    c_f = done("gs", g.iota(T.FL[:], [[0, R // Q]], 0, 2, **loose))
-
     def counts(bank, m, lo, hi, base):
-        wait("p", "gs", c_u)
         wait("p", "vs", count["vs"])
         out = bank[:, 0:hi - lo]
-        g.tensor.matmul(out, T.U[:], m[:, lo + 1:hi + 1], True, False)
+        g.tensor.matmul(out, T.U[:, 0:128], m[:, lo + 1:hi + 1], True, False)
         if base:
             g.tensor.matmul(out, T.ONE[0:1, :], T.BASE[0:1, lo:hi], False, False)
         return done("ps", g.tensor.matmul(out, T.U2[:], m[:, lo:hi], False, True))
@@ -254,6 +184,235 @@ def rank_program(g, core, T, topo):
     def last(out, cw):
         return V(g.vector.tensor_tensor(out[:, 0:cw - 1], T.R2[:, 0:cw - 1], T.R1[:, 2 * cw:3 * cw - 1], op.add))
 
+    def product(out, w, a, b, ready):
+        step = 4
+        for k in range(NT):
+            if k == NT - step:
+                step = 2
+            if k % step == 0:
+                v, s = ready[k + step - 1]
+                wait("p", "vs", v)
+                wait("p", "acs", s)
+            ins = g.tensor.matmul(out[0:w, 0:MS + 1], a(k), b(k), k == 0, k == NT - 1)
+        return done("ps", ins)
+
+    def differences(out, w, mark):
+        wait("v", "ps", mark)
+        V(g.vector.tensor_copy(T.OC[0:w, :], out[0:w, 0:MS]))
+        vself()
+        V(g.vector.tensor_tensor(T.DIF[0:w, :], T.OC[0:w, :], out[0:w, 1:MS + 1], op.subtract))
+        wait("p", "vs", count["vs"])
+
+    return wait, done, V, A, vself, counts, scans, merge, last, product, differences, count
+
+
+def relay_program(g, core, T, topo):
+    for rank in range(N):
+        mine = relays(T, topo, rank)
+        for i, (c, dests) in enumerate(mine):
+            if c == core:
+                serve(g, core, T, topo, rank, i, len(mine), dests)
+
+
+def serve(g, core, T, topo, rank, i, parts, dests):
+    op, fn, loose = AluOpType, ActivationFunctionType, {"allow_small_or_imprecise_dtypes": True}
+    wait, done, V, A, vself, counts, scans, merge, last, product, differences, count = tools(g, T)
+    src = T.cores[rank]
+    off, on = others(T, topo, rank)
+    whole = topo.mask(core, src)
+    away = topo.mask(src, T.cores[off[0]])
+    inside = topo.mask(src, core) & ~away
+    outside = topo.mask(core, T.cores[dests[0]])
+    masks, k = split(outside, len(dests))
+    helper = i == 0
+
+    n = 8 // parts
+    part = T.SEL[:, i * n * 128:(i + 1) * n * 128]
+    r0, r1 = (0, 8) if helper else (i * n, (i + 1) * n)
+    made = T.SEL[:, r0 * 128:r1 * 128]
+    wait("g", "vs", V(g.vector.memset(made, 0.5)))
+    sel = done("gs", g.affine_select(made, made, [[-Q, r1 - r0], [0, 8], [-1, Q]], op.is_equal, 0.0, -Q * r0, 1))
+    wait("g", "gs", sel)
+    g.remote_dma_fused([RemoteDMATransfer(dst_ids=[dst_id(topo, src, core)], dma_engine_mask=whole,
+                                          remote_sem=T.sem.cs, src=part, dst=part)], local_sem=T.sem.sx)
+    sent = len(bits(whole))
+
+    if helper:
+        done("gs", g.iota(T.CB2[:], [[-256, MS + 1]], 1, 0, **loose))
+        done("gs", g.iota(T.IOT[:], [[1, 128]], 0, 0, **loose))
+        c_a = done("gs", g.iota(T.C128[:], [[128, MS + 1]], 0, 0, **loose))
+        done("gs", g.iota(T.FH[:], [[2 * Q, R // Q]], 0, 0, **loose))
+        c_f = done("gs", g.iota(T.FL[:], [[0, R // Q]], 0, 2, **loose))
+        V(g.vector.memset(T.ONE[:], 1.0))
+        V(g.vector.memset(T.RST[:], 1.0))
+        V(g.vector.memset(T.M2[:], 0.0))
+        V(g.vector.memset(T.BASE[:], 0.0))
+        V(g.vector.memset(T.FC[:], -float(R + MID)))
+        V(g.vector.memset(T.MZ[:, 0:3 * CW], 0.0))
+        V(g.vector.memset(T.PW2[:, 0:3 * CW], 0.0))
+        vself()
+        V(g.vector.memset(T.RST[:, 0:MW:CW], 0.0))
+        for b in range(N):
+            V(g.vector.memset(T.BASE[:, b * CW:b * CW + 1], float(landed(b) - R - MID)))
+        g.vector.wait_ge(T.sem.cu, len(bits(away)))
+        g.tensor.wait_ge(T.sem.cu, len(bits(away)))
+        V(g.vector.tensor_scalar(T.U2[:], T.U[:, 0:128], -1.0, 1.0, op.mult, op.add))
+        wait("p", "vs", count["vs"])
+        wait("p", "gs", c_f)
+        c = R // Q
+        g.tensor.matmul(T.PKD[:, 0:c], T.SEL[0:Q, 0:128], T.FH[0:Q, :], True, False)
+        g.tensor.matmul(T.PKD[:, 0:c], T.ONE[0:1, :], T.FC[0:1, :], False, False)
+        done("ps", g.tensor.matmul(T.PKD[:, 0:c], T.SEL[0:Q, 0:128], T.FL[0:Q, :], False, True))
+
+        arrive = 0
+        for a in range(N):
+            out = topo.mask(T.cores[a], core)
+            if a not in off:
+                out &= ~topo.mask(T.cores[a], T.cores[off[0]])
+            arrive += len(bits(out))
+        g.vector.wait_ge(T.sem.la, arrive)
+        S, D = T.LAND[:, :, 0:LT], T.LAND[:, :, LT:2 * LT]
+        V(g.vector.tensor_scalar(T.DH[:], D, 12, None, op.arith_shift_right))
+        V(g.vector.tensor_scalar(T.SH[:], S, 12, None, op.arith_shift_right))
+        vself()
+        V(g.vector.tensor_scalar(T.NM[:], T.DH[:], float(rank), 256.0, op.not_equal, op.mult))
+        vself()
+        V(g.vector.tensor_tensor(T.X[:], T.SH[:], T.NM[:], op.add))
+        vself()
+        h, w = 3 * CW, MW - 1
+        marks = []
+        for bank, a0, lo, hi in ((T.PINC, 0, 0, h), (T.PO2, 3, h, w)):
+            for a in range(a0, a0 + 3):
+                for x, y, m in runs(rank, a):
+                    e = a * CW + 1 + x * LT
+                    V(g.vector.tensor_scalar(T.M2[:, e:e + m * LT], T.X[:, y * LT:(y + m) * LT], float(a), None,
+                                             op.is_equal))
+            marks.append(counts(bank, T.M2, lo, hi, True))
+        low = V(g.vector.tensor_scalar(T.LOW[:], D, R - 1, None, op.bitwise_and))
+        rem = V(g.vector.tensor_scalar(T.REM[:], D, 127, None, op.bitwise_and))
+        wait("v", "vs", low)
+        dlf = V(g.vector.tensor_copy(T.DLF[:], T.LOW[:]))
+        wait("v", "vs", rem)
+        V(g.vector.tensor_tensor(T.KEY[:], T.REM[:], T.NM[:], op.add))
+        scans(T.RST, h, w, marks)
+        second = count["vs"]
+        for out, a0 in ((T.MZ, 0), (T.PW2, 3)):
+            for a in range(a0, a0 + 3):
+                for x, y, m in runs(rank, a):
+                    e, o = a * CW + x * LT, (a - a0) * CW + y * LT
+                    V(g.vector.tensor_tensor(out[:, o:o + m * LT], T.M2[:, e + 1:e + 1 + m * LT], T.PZ[:, e:e + m * LT],
+                                             op.mult))
+            wait("v", "vs", second)
+        merge(CW)
+        last(T.VAL, CW)
+        vself()
+        wait("v", "gs", c_f)
+        wait("a", "gs", c_a)
+        wait("a", "vs", dlf)
+        ready = []
+        for t in range(NT):
+            if t % 8 == 1:
+                V(g.vector.tensor_scalar(T.B2[:, t, 0:MS + 1], T.C128[:], T.DLF[:, t:t + 1], 2.0, op.is_le, op.mult))
+            else:
+                A(g.scalar.activation(T.B2[:, t, 0:MS + 1], T.CB2[:], fn.Sign, bias=T.DLF[:, t:t + 1], scale=0.5))
+            V(g.vector.tensor_scalar(T.A2[:, t, :], T.IOT[:], T.KEY[:, t:t + 1], T.VAL[:, t:t + 1], op.is_equal, op.mult))
+            ready.append((count["vs"], count["acs"]))
+        mark = product(T.PO, 128, lambda t: T.A2[:, t, :], lambda t: T.B2[:, t, 0:MS + 1], ready)
+        differences(T.PO, 128, mark)
+        for r in range(8):
+            mark = done("ps", g.tensor.matmul(T.PW2[:, r:c:8], T.SEL[:, r * 128:(r + 1) * 128], T.DIF[:], True, True))
+        wait("v", "ps", mark)
+        V(g.vector.tensor_scalar(T.ADD[:], T.PW2[:, 0:c], 0.0, None, op.is_equal))
+        vself()
+        V(g.vector.tensor_tensor(T.ADD[:], T.ADD[:], T.PKD[:, 0:c], op.mult))
+        vself()
+        V(g.vector.tensor_tensor(T.ADD[:], T.ADD[:], T.PW2[:, 0:c], op.add))
+        vself()
+        V(g.vector.tensor_scalar(T.INV[:], T.ADD[:], float(R + MID), None, op.add))
+
+    to = landed(rank)
+    for j, (relay, now) in enumerate(turns(T, topo, rank)):
+        if relay != core:
+            continue
+        g.wait_ge(T.sem["rl%d" % j], len(bits(whole if j == 0 else inside)))
+        tr = []
+        for d in now:
+            e = dests.index(d)
+            tr.append(RemoteDMATransfer(dst_ids=[dst_id(topo, T.cores[d], core)], dma_engine_mask=masks[e],
+                                        remote_sem=T.sem["ra%d" % rank], src=T.RB[:, e, :], dst=T.TW[:, to:to + PR]))
+        g.remote_dma_fused(tr, local_sem=T.sem.sx)
+    sent += k * len(dests)
+    if helper:
+        near = whole & ~outside
+        wait("g", "vs", count["vs"])
+        g.remote_dma_fused([RemoteDMATransfer(dst_ids=[dst_id(topo, src, core)], dma_engine_mask=near,
+                                              remote_sem=T.sem.iv, src=T.INV[:], dst=T.INV[:])], local_sem=T.sem.sx)
+        sent += len(bits(near))
+        wait("g", "acs", count["acs"])
+        wait("g", "ps", count["ps"])
+    wait("g", "gs", count["gs"])
+    g.wait_ge(T.sem.sx, sent)
+
+
+def rank_program(g, core, T, topo):
+    me = T.rank_of(core)
+    if me is None:
+        return relay_program(g, core, T, topo)
+    op, fn = AluOpType, ActivationFunctionType
+    wait, done, V, A, vself, counts, scans, merge, last, product, differences, count = tools(g, T)
+    off, on = others(T, topo, me)
+    outside = topo.mask(core, T.cores[off[0]])
+    inside = topo.mask(core, T.cores[on[0]]) & ~outside
+    mine = relays(T, topo, me)
+    helper = helper_of(T, topo, me)
+    loose = {"allow_small_or_imprecise_dtypes": True}
+
+    g.sync.dma_start(T.LAND[:, 0, 0:LT], T.src[:]).then_inc(T.sem.ld, 16)
+    g.scalar.dma_start(T.LAND[:, 0, LT:2 * LT], T.dst[:]).then_inc(T.sem.ld, 16)
+    g.sync.dma_start(T.TW[:, 0:FIRST], T.tab[:, 0:FIRST]).then_inc(T.sem.tl, 16)
+
+    wait("g", "vs", V(g.vector.memset(T.U[:], 1.0)))
+    c_u = done("gs", g.affine_select(T.U[:], T.U[:], [[1, 129]], op.is_gt, 0.0, 0, -1))
+    wait("g", "gs", c_u)
+    g.remote_dma_fused([RemoteDMATransfer(dst_ids=[dst_id(topo, helper, core)], dma_engine_mask=outside,
+                                          remote_sem=T.sem.cu, src=T.U[:], dst=T.U[:])], local_sem=T.sem.sn)
+    sent = len(bits(outside))
+    V(g.vector.memset(T.ME[:], 0.0))
+    V(g.vector.memset(T.RSTE[:], 1.0))
+    V(g.vector.memset(T.M[:], 0.0))
+    V(g.vector.memset(T.RST[:], 1.0))
+    V(g.vector.memset(T.NZ[:], -0.0))
+    V(g.vector.memset(T.TW[:, R + MID:R + MID + GAP], 0.0))
+    vself()
+    V(g.vector.memset(T.RSTE[:, 0:MWE:CWE], 0.0))
+    V(g.vector.memset(T.RST[:, 0:MW:CW], 0.0))
+    wait("v", "gs", c_u)
+    V(g.vector.tensor_scalar(T.U2[:], T.U[:, 0:128], -1.0, 1.0, op.mult, op.add))
+    V(g.vector.tensor_tensor(T.IDENT[:], T.U[:, 1:129], T.U[:, 0:128], op.subtract))
+    V(g.vector.memset(T.POST[:], 1.0))
+    wait("p", "gs", c_u)
+
+    g.wait_ge(T.sem.ld, 32)
+    arrive = 0
+    for group, mask, to_ranks in ((off, outside, True), (on, inside, True), (off, outside, False),
+                                  (on + [me], inside, False)):
+        cores = [T.cores[d] if to_ranks else helper_of(T, topo, d) for d in group]
+        g.remote_dma_fused([RemoteDMATransfer(dst_ids=[dst_id(topo, c, core) for c in cores],
+                                              dma_engine_mask=mask, remote_sem=T.sem.la, srcs=[T.LAND[:, 0, :]],
+                                              dsts=[T.LAND[:, place(d, me), :] for d in group])], local_sem=T.sem.sn)
+        sent += len(bits(mask))
+        if to_ranks:
+            arrive += len(group) * len(bits(mask))
+    g.sem_inc(T.sem.go, 1)
+    g.sync.wait_ge(T.sem.go, 1)
+    g.sync.dma_start(T.TW[:, FIRST:R], T.tab[:, FIRST:R]).then_inc(T.sem.tl, 16)
+    c_a = done("gs", g.iota(T.IOT[:], [[1, 128]], 0, 0, **loose))
+    c_cb = done("gs", g.iota(T.CB[:], [[-2 * Q, MS + 1]], 1, 0, **loose))
+    flat, grid = [[0, BCH], [0, BW]], [[1, BCH], [0, BW]]
+    wait("g", "gs", done("gs", g.iota(T.EXP[:], [[0, BCH], [-Q, BW]], 0, 0, **loose)))
+    wait("g", "gs", done("gs", g.affine_select(T.EXP[:], T.EXP[:], flat, op.is_ge, 0.0, -BCH, 1)))
+    c_e = done("gs", g.affine_select(T.EXP[:], T.EXP[:], grid, op.not_equal, 1.0, 0, -1))
+
     def source_keys(lists, m, rst, pos):
         n = lists * LT
         cw = n + 1
@@ -271,84 +430,67 @@ def rank_program(g, core, T, topo):
             for b in range(b0, b0 + 3):
                 V(g.vector.tensor_scalar(m[:, b * cw + 1:b * cw + cw], T.X[:, 0:n], float(b), None, op.is_equal))
             marks.append(counts(bank, m, lo, hi, False))
-        low = V(g.vector.tensor_scalar(T.LOW[:, 0:n], S, R - 1, None, op.bitwise_and))
         V(g.vector.tensor_scalar(T.X16[:, 0:n], T.X[:, 0:n], float(Q), None, op.mult))
-        wait("v", "vs", low)
-        V(g.vector.tensor_scalar(T.VAL[:, 0:n], T.LOW[:, 0:n], -float(MID), None, op.add))
+        V(g.vector.tensor_scalar(T.VAL[:, 0:n], S, -float(R * me + MID), None, op.add))
         scans(rst, h, w, marks)
         second = count["vs"]
         V(g.vector.tensor_tensor(T.MZ[:, 0:h - 1], m[:, 1:h], T.PZ[:, 0:h - 1], op.mult))
         wait("v", "vs", second)
         V(g.vector.tensor_tensor(T.PW2[:, 0:h - 1], m[:, h + 1:w + 1], T.PZ[:, h:w], op.mult))
         merge(cw)
-        posi = last(T.POSI, cw)
-        wait("a", "vs", last(pos, cw))
-        wait("v", "vs", posi)
+        at = last(pos, cw)
+        last(T.POSI, cw)
+        vself()
         V(g.vector.tensor_scalar(T.REM[:, 0:n], T.POSI[:, 0:n], Q - 1, None, op.bitwise_and))
         vself()
         V(g.vector.tensor_tensor(T.KEY[:, 0:n], T.REM[:, 0:n], T.X16[:, 0:n], op.add))
         vself()
-
-    def rows(t0, t1, a, w, b, cb, cv, at, share):
-        ready = []
-        for t in range(t0, t1):
-            if t % share == 1:
-                V(g.vector.tensor_scalar(b[:, t, 0:MS + 1], cv[:], at[:, t:t + 1], 2.0, op.is_le, op.mult))
-            else:
-                A(g.scalar.activation(b[:, t, 0:MS + 1], cb[:], fn.Sign, bias=at[:, t:t + 1], scale=0.5))
-            V(g.vector.tensor_scalar(a[:, t, :], T.IOT[:, 0:w], T.KEY[:, t:t + 1], T.VAL[:, t:t + 1],
-                                     op.is_equal, op.mult))
-            ready.append((count["vs"], count["acs"]))
-        return ready
-
-    def product(out, w, a, b, ready):
-        step = 4
-        for t in range(NT):
-            if t == NT - step:
-                step = 2
-            if t % step == 0:
-                v, s = ready[t + step - 1]
-                wait("p", "vs", v)
-                wait("p", "acs", s)
-            ins = g.tensor.matmul(out[0:w, 0:MS + 1], a[:, t, :], b[:, t, 0:MS + 1], t == 0, t == NT - 1)
-        return done("ps", ins)
-
-    def differences(out, w, mark):
-        wait("v", "ps", mark)
-        V(g.vector.tensor_copy(T.OC[0:w, :], out[0:w, 0:MS]))
-        vself()
-        V(g.vector.tensor_tensor(T.DIF[0:w, :], T.OC[0:w, :], out[0:w, 1:MS + 1], op.subtract))
-        wait("p", "vs", count["vs"])
+        return at
 
     w1 = N * Q
     g.vector.wait_ge(T.sem.ld, 32)
-    source_keys(1, T.ME, T.RSTE, T.POSE)
-    V(g.vector.memset(T.ONE[:], 1.0))
-    V(g.vector.memset(T.NZ[:], -0.0))
-    V(g.vector.memset(T.M2[:], 0.0))
-    V(g.vector.memset(T.BASE[:], 0.0))
-    V(g.vector.memset(T.FC[:], -float(R + MID)))
-    V(g.vector.memset(T.TW[:, R + MID:R + MID + GAP], 0.0))
-    vself()
-    for b in range(N):
-        V(g.vector.memset(T.BASE[:, b * CW:b * CW + 1], float(landed(b) - R - MID)))
+    at = source_keys(1, T.ME, T.RSTE, T.POSE)
     wait("v", "gs", c_a)
     wait("a", "gs", c_cb)
-    ready = rows(0, LT, T.A1, w1, T.B1, T.CB, T.C16, T.POSE, 5)
+    wait("a", "vs", at)
+    ready = []
+
+    def hot(k):
+        return V(g.vector.tensor_scalar(T.A1[:, k, :], T.IOT[:, 0:w1], T.KEY[:, k:k + 1], T.VAL[:, k:k + 1],
+                                        op.is_equal, op.mult))
+
+    for k in range(LT):
+        s = A(g.scalar.activation(T.B1[:, k * BW:k * BW + MS + 1], T.CB[:], fn.Sign, bias=T.POSE[:, k:k + 1], scale=0.5))
+        ready.append((hot(k), s))
     g.vector.wait_ge(T.sem.la, arrive)
-    source_keys(N, T.M, T.RST, T.POS)
-    ready += rows(LT, NT, T.A1, w1, T.B1, T.CB, T.C16, T.POS, 5)
-    mark = product(T.PO, w1, T.A1, T.B1, ready)
-    D = T.LAND[:, :, LT:2 * LT]
-    nm = V(g.vector.tensor_scalar(T.NM[:], T.DH[:], float(me), 256.0, op.not_equal, op.mult))
-    V(g.vector.tensor_scalar(T.LOW[:], D, R - 1, None, op.bitwise_and))
-    V(g.vector.tensor_scalar(T.REM[:], D, 127, None, op.bitwise_and))
-    wait("v", "vs", nm)
-    V(g.vector.tensor_tensor(T.X[:], T.SH[:], T.NM[:], op.add))
+    at = source_keys(N, T.M, T.RST, T.POSH)
+    wait("p", "vs", at)
+    thirds = []
+    for i, bank in enumerate((T.PKD, T.PZ, T.PO2)):
+        k0, k1 = LT + i * BCH, min(NT, LT + (i + 1) * BCH)
+        thirds.append((k0, k1, bank, done("ps", g.tensor.matmul(bank[0:k1 - k0, 0:128], T.POSH[:, k0:k1], T.IDENT[:],
+                                                                True, True))))
+    turned = []
+    for i, (k0, k1, bank, mark) in enumerate(thirds):
+        wait("a", "ps", mark)
+        turned.append(A(g.scalar.activation(T.POST[0:k1 - k0, i * 128:(i + 1) * 128], bank[0:k1 - k0, 0:128], fn.Identity,
+                                            bias=-0.25)))
+    wait("p", "gs", c_e)
+    step = {}
+    for i, (bank, (k0, k1, _b, _m)) in enumerate(zip((T.PWO, T.PWN, T.PINC), thirds)):
+        wait("p", "acs", turned[i])
+        n = (k1 - k0) * BW
+        mark = done("ps", g.tensor.matmul(bank[:, 0:n], T.POST[0:BCH + 1, i * 128:(i + 1) * 128], T.EXP[0:BCH + 1, 0:n],
+                                          True, True))
+        wait("a", "ps", mark)
+        s = A(g.scalar.activation(T.B1[:, k0 * BW:k1 * BW], bank[:, 0:n], fn.Sign, bias=0.75))
+        for k in range(k0, k1):
+            step[k] = s
+    for k in range(LT, NT):
+        ready.append((hot(k), step[k]))
+    mark = product(T.PO, w1, lambda k: T.A1[:, k, :], lambda k: T.B1[:, k * BW:k * BW + MS + 1], ready)
     differences(T.PO, w1, mark)
-    dlf = V(g.vector.tensor_copy(T.DLF[:], T.LOW[:]))
-    V(g.vector.tensor_tensor(T.KEY[:], T.REM[:], T.NM[:], op.add))
-    g.tensor.wait_ge(T.sem.cs, len(mine) * len(bits(outside)))
+    g.tensor.wait_ge(T.sem.cs, len(mine) * len(bits(topo.mask(helper, core))))
     near = sorted(on + [me])
     marks = {}
     for ps, bs in ((T.PWO, off), (T.PWN, near)):
@@ -360,10 +502,6 @@ def rank_program(g, core, T, topo):
         wait("v", "ps", marks[bs[0]])
         ofs[bs[0]] = V(g.vector.tensor_scalar(T.OFS[:, bs[0] * MS:(bs[-1] + 1) * MS], ps[:, 0:len(bs) * MS],
                                               float(MID), None, op.add))
-    wait("p", "gs", c_f)
-    g.tensor.matmul(T.PKD[:, 0:R // Q], T.SEL[0:Q, 0:128], T.FH[0:Q, :], True, False)
-    g.tensor.matmul(T.PKD[:, 0:R // Q], T.ONE[0:1, :], T.FC[0:1, :], False, False)
-    pkd = done("ps", g.tensor.matmul(T.PKD[:, 0:R // Q], T.SEL[0:Q, 0:128], T.FL[0:Q, :], False, True))
 
     def pick(eng, out, win):
         if eng == "v":
@@ -388,12 +526,15 @@ def rank_program(g, core, T, topo):
         wait(q, "tl", 32)
     got = {}
     feed = turns(T, topo, me)
-    for bs, s0, s1 in ((feed[0][1], 0, PR), (off, PR, CAPP), (feed[1][1], 0, PR)):
+    direct = pairs_of(off)
+    order = [(feed[0][1], 0, PR), (direct[0], PR, CAPP), (feed[1][1], 0, PR)] + [(bs, PR, CAPP) for bs in direct[1:]]
+    for bs, s0, s1 in order:
         for b in bs:
             got[(b, s0)] = gather("va"[off.index(b) % 2], b, s0, s1)
-    wait("a", "vs", ofs[near[0]])
-    for b in on + [me]:
-        got[b] = gather("a", b, 0, CAPP)
+    for q in ("v", "a"):
+        wait(q, "vs", ofs[near[0]])
+    for i, b in enumerate(on + [me]):
+        got[b] = gather("va"[i % 2], b, 0, CAPP)
 
     def send(marks, items, mask):
         wait("g", "vs", max(m[0] for m in marks))
@@ -405,65 +546,29 @@ def rank_program(g, core, T, topo):
 
     for j, (c, now) in enumerate(feed):
         i, e, n = off.index(now[0]), dict(mine)[c].index(now[0]), len(now)
-        send([got[(b, 0)] for b in now], [(c, "rl%d" % j, T.SREL[:, i:i + n, :], T.RB[:, e:e + n, :])], inside)
-        if j == 0:
-            send([got[(b, PR)] for b in off],
-                 [(T.cores[b], "rb%d" % me, T.SEND[:, b, PR:CAPP], T.TW[:, to + PR:to + CAPP]) for b in off], outside)
+        send([got[(b, 0)] for b in now], [(c, "rl%d" % j, T.SREL[:, i:i + n, :], T.RB[:, e:e + n, :])],
+             inside if j else inside | outside)
+        for bs in direct[j:j + 1]:
+            send([got[(b, PR)] for b in bs],
+                 [(T.cores[b], "rb%d" % me, T.SEND[:, b, PR:CAPP], T.TW[:, to + PR:to + CAPP]) for b in bs], outside)
     for now in portions(on):
         send([got[b] for b in now],
              [(T.cores[b], "rc%d" % me, T.SEND[:, b, :], T.TW[:, to:to + CAPP]) for b in now], inside)
 
-    h, w = 3 * CW, MW - 1
-    vself()
-    marks = []
-    for bank, a0, lo, hi in ((T.PINC, 0, 0, h), (T.PO2, 3, h, w)):
-        for a in range(a0, a0 + 3):
-            for i, j, n in runs(me, a):
-                c = a * CW + 1 + i * LT
-                V(g.vector.tensor_scalar(T.M2[:, c:c + n * LT], T.X[:, j * LT:(j + n) * LT], float(a), None, op.is_equal))
-        marks.append(counts(bank, T.M2, lo, hi, True))
-    scans(T.RST, h, w, marks)
-    second = count["vs"]
-    for out, a0 in ((T.MZ, 0), (T.PW2, 3)):
-        for a in range(a0, a0 + 3):
-            for i, j, n in runs(me, a):
-                c, o = a * CW + i * LT, (a - a0) * CW + j * LT
-                V(g.vector.tensor_tensor(out[:, o:o + n * LT], T.M2[:, c + 1:c + 1 + n * LT], T.PZ[:, c:c + n * LT], op.mult))
-        wait("v", "vs", second)
-    merge(CW)
-    last(T.VAL, CW)
-    vself()
-    wait("v", "gs", c_f)
-    wait("a", "gs", c_f)
-    wait("a", "vs", dlf)
-    ready = rows(0, NT, T.A2, 128, T.B2, T.CB2, T.C128, T.DLF, 8)
-    mark = product(T.PO2, 128, T.A2, T.B2, ready)
-    differences(T.PO2, 128, mark)
-    c = R // Q
-    for r in range(8):
-        mark = done("ps", g.tensor.matmul(T.PW2[:, r:c:8], T.SEL[:, r * 128:(r + 1) * 128], T.DIF[:], True, True))
-    wait("v", "ps", mark)
-    V(g.vector.tensor_scalar(T.ADD[:], T.PW2[:, 0:c], 0.0, None, op.is_equal))
-    vself()
-    V(g.vector.tensor_tensor(T.ADD[:], T.ADD[:], T.PKD[:, 0:c], op.mult))
-    vself()
-    V(g.vector.tensor_tensor(T.ADD[:], T.ADD[:], T.PW2[:, 0:c], op.add))
-    vself()
-    inv = V(g.vector.tensor_scalar(T.INV[:], T.ADD[:], float(R + MID), None, op.add))
-
-    arrivals = []
+    arrivals = [("iv", len(bits(topo.mask(helper, core) & ~topo.mask(helper, T.cores[off[0]]))))]
     for a in on:
         o = others(T, topo, a)
         inside_a = topo.mask(T.cores[a], core) & ~topo.mask(T.cores[a], T.cores[o[0][0]])
         run = [p for p in portions(o[1]) if me in p][0]
         arrivals.append(("rc%d" % a, split(inside_a, len(run))[1]))
     for a in off:
-        arrivals.append(("rb%d" % a, split(topo.mask(T.cores[a], core), len(others(T, topo, a)[0]))[1]))
+        run = [p for p in pairs_of(others(T, topo, a)[0]) if me in p][0]
+        arrivals.append(("rb%d" % a, split(topo.mask(T.cores[a], core), len(run))[1]))
         for c, dests in relays(T, topo, a):
             if me in dests:
                 arrivals.append(("ra%d" % a, split(topo.mask(c, core), len(dests))[1]))
     wait("v", "acs", count["acs"])
-    wait("a", "vs", inv)
+    wait("a", "vs", count["vs"])
     wait("a", "acs", count["acs"])
     vself()
     for q in ("v", "a"):
@@ -480,6 +585,6 @@ def rank_program(g, core, T, topo):
         c += n
     g.wait_ge(T.sem.sx, count["sx"])
     g.wait_ge(T.sem.sn, sent)
-    g.sync.wait_ge(T.sem.gs, count["gs"])
-    g.sync.wait_ge(T.sem.ps, count["ps"])
+    wait("s", "gs", count["gs"])
+    wait("s", "ps", count["ps"])
     g.sync.wait_ge(T.sem.st, 16 * len(YBLOCKS))

from concourse.bass import DstId, RemoteDMATransfer
from concourse.mybir import AluOpType, ActivationFunctionType

N, R, L, CAPP = 6, 4096, 1024, 512
SIM_CORES = 256
LT = L // 128
NT = N * LT
CW = NT + 1
MW = N * CW
CWE = LT + 1
MWE = N * CWE
Q = 16
MS = CAPP // Q
BW = MS + 2
BCH = -(-(NT - LT) // 3)
PR = 224
PAIR = 2
MID = R // 2
GAP = 4
WIN = R + N * CAPP + GAP
FIRST = 1024
YBLOCKS = [256, 512, 896, 1152, 1280]


def sbuf(dtype, *shape):
    return ("sbuf", [128] + list(shape), dtype)


SCRATCH = {
    "LAND": sbuf("int32", N, 2 * LT),
    "M": sbuf("bfloat16", MW), "RST": sbuf("float32", MW), "ME": sbuf("bfloat16", MWE), "RSTE": sbuf("float32", MWE),
    "M2": sbuf("bfloat16", MW), "BASE": sbuf("bfloat16", MW), "ONE": sbuf("bfloat16", 128),
    "U": sbuf("bfloat16", 129), "U2": sbuf("bfloat16", 128), "SEL": sbuf("bfloat16", 8 * 128),
    "IDENT": sbuf("bfloat16", 128), "POSH": sbuf("float16", NT),
    "EXP": sbuf("bfloat16", BCH * BW), "POST": sbuf("bfloat16", 3 * 128),
    "MZ": sbuf("float32", MW), "R1": sbuf("float32", 3 * CW), "R2": sbuf("float32", NT),
    "SH": sbuf("int32", NT), "DH": sbuf("int32", NT), "LOW": sbuf("int32", NT), "POSI": sbuf("int32", NT),
    "REM": sbuf("int32", NT), "NM": sbuf("float32", NT), "X": sbuf("float32", NT), "X16": sbuf("float32", NT),
    "KEY": sbuf("float32", NT), "VAL": sbuf("float32", NT),
    "POSE": sbuf("float32", LT), "DLF": sbuf("float32", NT),
    "IOT": sbuf("bfloat16", 128), "CB": sbuf("float32", MS + 1), "CB2": sbuf("float32", MS + 1),
    "C128": sbuf("bfloat16", MS + 1),
    "FH": sbuf("bfloat16", R // Q), "FL": sbuf("bfloat16", R // Q), "FC": sbuf("bfloat16", R // Q),
    "NZ": sbuf("float32", 1),
    "A1": sbuf("float16", NT, N * Q), "A2": sbuf("float16", NT, 128),
    "B1": sbuf("bfloat16", NT * BW), "B2": sbuf("bfloat16", NT, MS + 2),
    "OC": sbuf("float32", MS), "DIF": sbuf("float16", MS), "ADD": sbuf("float32", R // Q),
    "OFS": sbuf("uint16", N * MS), "INV": sbuf("uint16", R // Q),
    "TW": sbuf("float32", WIN), "YB": sbuf("float32", R),
    "SREL": sbuf("float32", N, PR), "SEND": sbuf("float32", N, CAPP), "RB": sbuf("float32", 2, PR),
}
for _k in ("PINC", "PZ", "PO", "PWO", "PWN", "PO2", "PW2", "PKD"):
    SCRATCH[_k] = ("psum", [128, 512], "float32")
SEMAPHORES = (["ld", "go", "tl", "la", "sn", "sx", "st", "gs", "vs", "acs", "ps", "cs", "rl0", "rl1", "iv", "cu"]
              + ["r%s%d" % (p, a) for p in "abc" for a in range(N)])


def same_chip(topo, a, b):
    return topo.host(a) == topo.host(b) and topo.chip(a) == topo.chip(b)


def others(T, topo, rank):
    c = T.cores[rank]
    off = [d for d in range(N) if not same_chip(topo, T.cores[d], c)]
    on = [d for d in range(N) if d != rank and d not in off]
    return off, on


def relays(T, topo, rank):
    c = T.cores[rank]
    peers = [x for x in T.cores if same_chip(topo, x, c)]
    cand = [x for x in range(SIM_CORES) if same_chip(topo, x, c) and topo.die(x) != topo.die(c) and x not in T.cores]
    off, _ = others(T, topo, rank)
    k = len(cand) // len(peers)
    i = peers.index(c)
    mine = cand[i * k:(i + 1) * k]
    m = len(off) // k
    return [(mine[j], off[j * m:(j + 1) * m]) for j in range(k)]


def helper_of(T, topo, rank):
    return relays(T, topo, rank)[0][0]


def turns(T, topo, rank):
    r = relays(T, topo, rank)
    return r if len(r) > 1 else [(c, [d]) for c, ds in r for d in ds]


def bits(mask):
    return [1 << i for i in range(16) if (mask >> i) & 1]


def split(mask, n):
    b = bits(mask)
    k = 1
    while 2 * k * n <= len(b):
        k *= 2
    return [sum(b[j * k:(j + 1) * k]) for j in range(n)], k


def portions(items):
    out, todo = [], list(items)
    while todo:
        n = 1
        while 2 * n <= len(todo):
            n *= 2
        out.append(todo[:n])
        todo = todo[n:]
    return out


def pairs_of(off):
    return [off[i:i + PAIR] for i in range(0, len(off), PAIR)]


def place(r, c):
    return (c - r) % N


def runs(r, a):
    d = (a - r) % N
    return [(0, d, N - d), (N - d, 0, d)] if d else [(0, 0, N)]


def landed(a):
    return R + a * CAPP + (GAP if a * CAPP >= MID else 0)


def dst_id(topo, dst, src):
    rid, pid = topo.addr(dst, src)
    return DstId(rid=rid, pnc=pid)


def tools(g, T):
    op = AluOpType
    queue = {"g": g, "v": g.vector, "a": g.scalar, "p": g.tensor, "s": g.sync}
    count = {"gs": 0, "vs": 0, "acs": 0, "ps": 0, "sx": 0}
    seen = {}

    def wait(q, sem, val):
        if seen.get((q, sem), 0) < val:
            seen[(q, sem)] = val
            queue[q].wait_ge(T.sem[sem], val)

    def done(sem, ins):
        ins.then_inc(T.sem[sem], 1)
        count[sem] += 1
        return count[sem]

    def V(ins):
        return done("vs", ins)

    def A(ins):
        return done("acs", ins)

    def vself():
        wait("v", "vs", count["vs"])

    def counts(bank, m, lo, hi, base):
        wait("p", "vs", count["vs"])
        out = bank[:, 0:hi - lo]
        g.tensor.matmul(out, T.U[:, 0:128], m[:, lo + 1:hi + 1], True, False)
        if base:
            g.tensor.matmul(out, T.ONE[0:1, :], T.BASE[0:1, lo:hi], False, False)
        return done("ps", g.tensor.matmul(out, T.U2[:], m[:, lo:hi], False, True))

    def scans(rst, h, w, marks):
        wait("v", "ps", marks[0])
        V(g.vector.tensor_tensor_scan(T.PZ[:, 0:h], rst[:, 0:h], T.PINC[:, 0:h], 0.0, op.mult, op.add))
        first = count["vs"]
        wait("v", "ps", marks[1])
        V(g.vector.tensor_tensor_scan(T.PZ[:, h:w], rst[:, h:w], T.PO2[:, 0:w - h], 0.0, op.mult, op.add))
        wait("v", "vs", first)

    def merge(cw):
        w = 3 * cw - 1
        vself()
        V(g.vector.tensor_tensor(T.R1[:, 0:w], T.MZ[:, 0:w], T.PW2[:, 0:w], op.add))
        vself()
        V(g.vector.tensor_tensor(T.R2[:, 0:cw - 1], T.R1[:, 0:cw - 1], T.R1[:, cw:2 * cw - 1], op.add))
        vself()

    def last(out, cw):
        return V(g.vector.tensor_tensor(out[:, 0:cw - 1], T.R2[:, 0:cw - 1], T.R1[:, 2 * cw:3 * cw - 1], op.add))

    def product(out, w, a, b, ready):
        step = 4
        for k in range(NT):
            if k == NT - step:
                step = 2
            if k % step == 0:
                v, s = ready[k + step - 1]
                wait("p", "vs", v)
                wait("p", "acs", s)
            ins = g.tensor.matmul(out[0:w, 0:MS + 1], a(k), b(k), k == 0, k == NT - 1)
        return done("ps", ins)

    def differences(out, w, mark):
        wait("v", "ps", mark)
        V(g.vector.tensor_copy(T.OC[0:w, :], out[0:w, 0:MS]))
        vself()
        V(g.vector.tensor_tensor(T.DIF[0:w, :], T.OC[0:w, :], out[0:w, 1:MS + 1], op.subtract))
        wait("p", "vs", count["vs"])

    return wait, done, V, A, vself, counts, scans, merge, last, product, differences, count


def relay_program(g, core, T, topo):
    for rank in range(N):
        mine = relays(T, topo, rank)
        for i, (c, dests) in enumerate(mine):
            if c == core:
                serve(g, core, T, topo, rank, i, len(mine), dests)


def serve(g, core, T, topo, rank, i, parts, dests):
    op, fn, loose = AluOpType, ActivationFunctionType, {"allow_small_or_imprecise_dtypes": True}
    wait, done, V, A, vself, counts, scans, merge, last, product, differences, count = tools(g, T)
    src = T.cores[rank]
    off, on = others(T, topo, rank)
    whole = topo.mask(core, src)
    away = topo.mask(src, T.cores[off[0]])
    inside = topo.mask(src, core) & ~away
    outside = topo.mask(core, T.cores[dests[0]])
    masks, k = split(outside, len(dests))
    helper = i == 0

    n = 8 // parts
    part = T.SEL[:, i * n * 128:(i + 1) * n * 128]
    r0, r1 = (0, 8) if helper else (i * n, (i + 1) * n)
    made = T.SEL[:, r0 * 128:r1 * 128]
    wait("g", "vs", V(g.vector.memset(made, 0.5)))
    sel = done("gs", g.affine_select(made, made, [[-Q, r1 - r0], [0, 8], [-1, Q]], op.is_equal, 0.0, -Q * r0, 1))
    wait("g", "gs", sel)
    g.remote_dma_fused([RemoteDMATransfer(dst_ids=[dst_id(topo, src, core)], dma_engine_mask=whole,
                                          remote_sem=T.sem.cs, src=part, dst=part)], local_sem=T.sem.sx)
    sent = len(bits(whole))

    if helper:
        done("gs", g.iota(T.CB2[:], [[-256, MS + 1]], 1, 0, **loose))
        done("gs", g.iota(T.IOT[:], [[1, 128]], 0, 0, **loose))
        c_a = done("gs", g.iota(T.C128[:], [[128, MS + 1]], 0, 0, **loose))
        done("gs", g.iota(T.FH[:], [[2 * Q, R // Q]], 0, 0, **loose))
        c_f = done("gs", g.iota(T.FL[:], [[0, R // Q]], 0, 2, **loose))
        V(g.vector.memset(T.ONE[:], 1.0))
        V(g.vector.memset(T.RST[:], 1.0))
        V(g.vector.memset(T.M2[:], 0.0))
        V(g.vector.memset(T.BASE[:], 0.0))
        V(g.vector.memset(T.FC[:], -float(R + MID)))
        V(g.vector.memset(T.MZ[:, 0:3 * CW], 0.0))
        V(g.vector.memset(T.PW2[:, 0:3 * CW], 0.0))
        vself()
        V(g.vector.memset(T.RST[:, 0:MW:CW], 0.0))
        for b in range(N):
            V(g.vector.memset(T.BASE[:, b * CW:b * CW + 1], float(landed(b) - R - MID)))
        g.vector.wait_ge(T.sem.cu, len(bits(away)))
        g.tensor.wait_ge(T.sem.cu, len(bits(away)))
        V(g.vector.tensor_scalar(T.U2[:], T.U[:, 0:128], -1.0, 1.0, op.mult, op.add))
        wait("p", "vs", count["vs"])
        wait("p", "gs", c_f)
        c = R // Q
        g.tensor.matmul(T.PKD[:, 0:c], T.SEL[0:Q, 0:128], T.FH[0:Q, :], True, False)
        g.tensor.matmul(T.PKD[:, 0:c], T.ONE[0:1, :], T.FC[0:1, :], False, False)
        done("ps", g.tensor.matmul(T.PKD[:, 0:c], T.SEL[0:Q, 0:128], T.FL[0:Q, :], False, True))

        arrive = 0
        for a in range(N):
            out = topo.mask(T.cores[a], core)
            if a not in off:
                out &= ~topo.mask(T.cores[a], T.cores[off[0]])
            arrive += len(bits(out))
        g.vector.wait_ge(T.sem.la, arrive)
        S, D = T.LAND[:, :, 0:LT], T.LAND[:, :, LT:2 * LT]
        V(g.vector.tensor_scalar(T.DH[:], D, 12, None, op.arith_shift_right))
        V(g.vector.tensor_scalar(T.SH[:], S, 12, None, op.arith_shift_right))
        vself()
        V(g.vector.tensor_scalar(T.NM[:], T.DH[:], float(rank), 256.0, op.not_equal, op.mult))
        vself()
        V(g.vector.tensor_tensor(T.X[:], T.SH[:], T.NM[:], op.add))
        vself()
        h, w = 3 * CW, MW - 1
        marks = []
        for bank, a0, lo, hi in ((T.PINC, 0, 0, h), (T.PO2, 3, h, w)):
            for a in range(a0, a0 + 3):
                for x, y, m in runs(rank, a):
                    e = a * CW + 1 + x * LT
                    V(g.vector.tensor_scalar(T.M2[:, e:e + m * LT], T.X[:, y * LT:(y + m) * LT], float(a), None,
                                             op.is_equal))
            marks.append(counts(bank, T.M2, lo, hi, True))
        low = V(g.vector.tensor_scalar(T.LOW[:], D, R - 1, None, op.bitwise_and))
        rem = V(g.vector.tensor_scalar(T.REM[:], D, 127, None, op.bitwise_and))
        wait("v", "vs", low)
        dlf = V(g.vector.tensor_copy(T.DLF[:], T.LOW[:]))
        wait("v", "vs", rem)
        V(g.vector.tensor_tensor(T.KEY[:], T.REM[:], T.NM[:], op.add))
        scans(T.RST, h, w, marks)
        second = count["vs"]
        for out, a0 in ((T.MZ, 0), (T.PW2, 3)):
            for a in range(a0, a0 + 3):
                for x, y, m in runs(rank, a):
                    e, o = a * CW + x * LT, (a - a0) * CW + y * LT
                    V(g.vector.tensor_tensor(out[:, o:o + m * LT], T.M2[:, e + 1:e + 1 + m * LT], T.PZ[:, e:e + m * LT],
                                             op.mult))
            wait("v", "vs", second)
        merge(CW)
        last(T.VAL, CW)
        vself()
        wait("v", "gs", c_f)
        wait("a", "gs", c_a)
        wait("a", "vs", dlf)
        ready = []
        for t in range(NT):
            if t % 8 == 1:
                V(g.vector.tensor_scalar(T.B2[:, t, 0:MS + 1], T.C128[:], T.DLF[:, t:t + 1], 2.0, op.is_le, op.mult))
            else:
                A(g.scalar.activation(T.B2[:, t, 0:MS + 1], T.CB2[:], fn.Sign, bias=T.DLF[:, t:t + 1], scale=0.5))
            V(g.vector.tensor_scalar(T.A2[:, t, :], T.IOT[:], T.KEY[:, t:t + 1], T.VAL[:, t:t + 1], op.is_equal, op.mult))
            ready.append((count["vs"], count["acs"]))
        mark = product(T.PO, 128, lambda t: T.A2[:, t, :], lambda t: T.B2[:, t, 0:MS + 1], ready)
        differences(T.PO, 128, mark)
        for r in range(8):
            mark = done("ps", g.tensor.matmul(T.PW2[:, r:c:8], T.SEL[:, r * 128:(r + 1) * 128], T.DIF[:], True, True))
        wait("v", "ps", mark)
        V(g.vector.tensor_scalar(T.ADD[:], T.PW2[:, 0:c], 0.0, None, op.is_equal))
        vself()
        V(g.vector.tensor_tensor(T.ADD[:], T.ADD[:], T.PKD[:, 0:c], op.mult))
        vself()
        V(g.vector.tensor_tensor(T.ADD[:], T.ADD[:], T.PW2[:, 0:c], op.add))
        vself()
        V(g.vector.tensor_scalar(T.INV[:], T.ADD[:], float(R + MID), None, op.add))

    to = landed(rank)
    for j, (relay, now) in enumerate(turns(T, topo, rank)):
        if relay != core:
            continue
        g.wait_ge(T.sem["rl%d" % j], len(bits(whole if j == 0 else inside)))
        tr = []
        for d in now:
            e = dests.index(d)
            tr.append(RemoteDMATransfer(dst_ids=[dst_id(topo, T.cores[d], core)], dma_engine_mask=masks[e],
                                        remote_sem=T.sem["ra%d" % rank], src=T.RB[:, e, :], dst=T.TW[:, to:to + PR]))
        g.remote_dma_fused(tr, local_sem=T.sem.sx)
    sent += k * len(dests)
    if helper:
        near = whole & ~outside
        wait("g", "vs", count["vs"])
        g.remote_dma_fused([RemoteDMATransfer(dst_ids=[dst_id(topo, src, core)], dma_engine_mask=near,
                                              remote_sem=T.sem.iv, src=T.INV[:], dst=T.INV[:])], local_sem=T.sem.sx)
        sent += len(bits(near))
        wait("g", "acs", count["acs"])
        wait("g", "ps", count["ps"])
    wait("g", "gs", count["gs"])
    g.wait_ge(T.sem.sx, sent)


def rank_program(g, core, T, topo):
    me = T.rank_of(core)
    if me is None:
        return relay_program(g, core, T, topo)
    op, fn = AluOpType, ActivationFunctionType
    wait, done, V, A, vself, counts, scans, merge, last, product, differences, count = tools(g, T)
    off, on = others(T, topo, me)
    outside = topo.mask(core, T.cores[off[0]])
    inside = topo.mask(core, T.cores[on[0]]) & ~outside
    mine = relays(T, topo, me)
    helper = helper_of(T, topo, me)
    loose = {"allow_small_or_imprecise_dtypes": True}

    g.sync.dma_start(T.LAND[:, 0, 0:LT], T.src[:]).then_inc(T.sem.ld, 16)
    g.scalar.dma_start(T.LAND[:, 0, LT:2 * LT], T.dst[:]).then_inc(T.sem.ld, 16)
    g.sync.dma_start(T.TW[:, 0:FIRST], T.tab[:, 0:FIRST]).then_inc(T.sem.tl, 16)

    wait("g", "vs", V(g.vector.memset(T.U[:], 1.0)))
    c_u = done("gs", g.affine_select(T.U[:], T.U[:], [[1, 129]], op.is_gt, 0.0, 0, -1))
    wait("g", "gs", c_u)
    g.remote_dma_fused([RemoteDMATransfer(dst_ids=[dst_id(topo, helper, core)], dma_engine_mask=outside,
                                          remote_sem=T.sem.cu, src=T.U[:], dst=T.U[:])], local_sem=T.sem.sn)
    sent = len(bits(outside))
    V(g.vector.memset(T.ME[:], 0.0))
    V(g.vector.memset(T.RSTE[:], 1.0))
    V(g.vector.memset(T.M[:], 0.0))
    V(g.vector.memset(T.RST[:], 1.0))
    V(g.vector.memset(T.NZ[:], -0.0))
    V(g.vector.memset(T.TW[:, R + MID:R + MID + GAP], 0.0))
    vself()
    V(g.vector.memset(T.RSTE[:, 0:MWE:CWE], 0.0))
    V(g.vector.memset(T.RST[:, 0:MW:CW], 0.0))
    wait("v", "gs", c_u)
    V(g.vector.tensor_scalar(T.U2[:], T.U[:, 0:128], -1.0, 1.0, op.mult, op.add))
    V(g.vector.tensor_tensor(T.IDENT[:], T.U[:, 1:129], T.U[:, 0:128], op.subtract))
    V(g.vector.memset(T.POST[:], 1.0))
    wait("p", "gs", c_u)

    g.wait_ge(T.sem.ld, 32)
    arrive = 0
    for group, mask, to_ranks in ((off, outside, True), (on, inside, True), (off, outside, False),
                                  (on + [me], inside, False)):
        cores = [T.cores[d] if to_ranks else helper_of(T, topo, d) for d in group]
        g.remote_dma_fused([RemoteDMATransfer(dst_ids=[dst_id(topo, c, core) for c in cores],
                                              dma_engine_mask=mask, remote_sem=T.sem.la, srcs=[T.LAND[:, 0, :]],
                                              dsts=[T.LAND[:, place(d, me), :] for d in group])], local_sem=T.sem.sn)
        sent += len(bits(mask))
        if to_ranks:
            arrive += len(group) * len(bits(mask))
    g.sem_inc(T.sem.go, 1)
    g.sync.wait_ge(T.sem.go, 1)
    g.sync.dma_start(T.TW[:, FIRST:R], T.tab[:, FIRST:R]).then_inc(T.sem.tl, 16)
    c_a = done("gs", g.iota(T.IOT[:], [[1, 128]], 0, 0, **loose))
    c_cb = done("gs", g.iota(T.CB[:], [[-2 * Q, MS + 1]], 1, 0, **loose))
    flat, grid = [[0, BCH], [0, BW]], [[1, BCH], [0, BW]]
    wait("g", "gs", done("gs", g.iota(T.EXP[:], [[0, BCH], [-Q, BW]], 0, 0, **loose)))
    wait("g", "gs", done("gs", g.affine_select(T.EXP[:], T.EXP[:], flat, op.is_ge, 0.0, -BCH, 1)))
    c_e = done("gs", g.affine_select(T.EXP[:], T.EXP[:], grid, op.not_equal, 1.0, 0, -1))

    def source_keys(lists, m, rst, pos):
        n = lists * LT
        cw = n + 1
        h, w = 3 * cw, 6 * cw - 1
        S, D = T.LAND[:, 0:lists, 0:LT], T.LAND[:, 0:lists, LT:2 * LT]
        V(g.vector.tensor_scalar(T.SH[:, 0:n], S, 12, None, op.arith_shift_right))
        V(g.vector.tensor_scalar(T.DH[:, 0:n], D, 12, None, op.arith_shift_right))
        vself()
        V(g.vector.tensor_scalar(T.NM[:, 0:n], T.SH[:, 0:n], float(me), 64.0, op.not_equal, op.mult))
        vself()
        V(g.vector.tensor_tensor(T.X[:, 0:n], T.DH[:, 0:n], T.NM[:, 0:n], op.add))
        vself()
        marks = []
        for bank, b0, lo, hi in ((T.PINC, 0, 0, h), (T.PO2, 3, h, w)):
            for b in range(b0, b0 + 3):
                V(g.vector.tensor_scalar(m[:, b * cw + 1:b * cw + cw], T.X[:, 0:n], float(b), None, op.is_equal))
            marks.append(counts(bank, m, lo, hi, False))
        V(g.vector.tensor_scalar(T.X16[:, 0:n], T.X[:, 0:n], float(Q), None, op.mult))
        V(g.vector.tensor_scalar(T.VAL[:, 0:n], S, -float(R * me + MID), None, op.add))
        scans(rst, h, w, marks)
        second = count["vs"]
        V(g.vector.tensor_tensor(T.MZ[:, 0:h - 1], m[:, 1:h], T.PZ[:, 0:h - 1], op.mult))
        wait("v", "vs", second)
        V(g.vector.tensor_tensor(T.PW2[:, 0:h - 1], m[:, h + 1:w + 1], T.PZ[:, h:w], op.mult))
        merge(cw)
        at = last(pos, cw)
        last(T.POSI, cw)
        vself()
        V(g.vector.tensor_scalar(T.REM[:, 0:n], T.POSI[:, 0:n], Q - 1, None, op.bitwise_and))
        vself()
        V(g.vector.tensor_tensor(T.KEY[:, 0:n], T.REM[:, 0:n], T.X16[:, 0:n], op.add))
        vself()
        return at

    w1 = N * Q
    g.vector.wait_ge(T.sem.ld, 32)
    at = source_keys(1, T.ME, T.RSTE, T.POSE)
    wait("v", "gs", c_a)
    wait("a", "gs", c_cb)
    wait("a", "vs", at)
    ready = []

    def hot(k):
        return V(g.vector.tensor_scalar(T.A1[:, k, :], T.IOT[:, 0:w1], T.KEY[:, k:k + 1], T.VAL[:, k:k + 1],
                                        op.is_equal, op.mult))

    for k in range(LT):
        s = A(g.scalar.activation(T.B1[:, k * BW:k * BW + MS + 1], T.CB[:], fn.Sign, bias=T.POSE[:, k:k + 1], scale=0.5))
        ready.append((hot(k), s))
    g.vector.wait_ge(T.sem.la, arrive)
    at = source_keys(N, T.M, T.RST, T.POSH)
    wait("p", "vs", at)
    thirds = []
    for i, bank in enumerate((T.PKD, T.PZ, T.PO2)):
        k0, k1 = LT + i * BCH, min(NT, LT + (i + 1) * BCH)
        thirds.append((k0, k1, bank, done("ps", g.tensor.matmul(bank[0:k1 - k0, 0:128], T.POSH[:, k0:k1], T.IDENT[:],
                                                                True, True))))
    turned = []
    for i, (k0, k1, bank, mark) in enumerate(thirds):
        wait("a", "ps", mark)
        turned.append(A(g.scalar.activation(T.POST[0:k1 - k0, i * 128:(i + 1) * 128], bank[0:k1 - k0, 0:128], fn.Identity,
                                            bias=-0.25)))
    wait("p", "gs", c_e)
    step = {}
    for i, (bank, (k0, k1, _b, _m)) in enumerate(zip((T.PWO, T.PWN, T.PINC), thirds)):
        wait("p", "acs", turned[i])
        n = (k1 - k0) * BW
        mark = done("ps", g.tensor.matmul(bank[:, 0:n], T.POST[0:BCH + 1, i * 128:(i + 1) * 128], T.EXP[0:BCH + 1, 0:n],
                                          True, True))
        wait("a", "ps", mark)
        s = A(g.scalar.activation(T.B1[:, k0 * BW:k1 * BW], bank[:, 0:n], fn.Sign, bias=0.75))
        for k in range(k0, k1):
            step[k] = s
    for k in range(LT, NT):
        ready.append((hot(k), step[k]))
    mark = product(T.PO, w1, lambda k: T.A1[:, k, :], lambda k: T.B1[:, k * BW:k * BW + MS + 1], ready)
    differences(T.PO, w1, mark)
    g.tensor.wait_ge(T.sem.cs, len(mine) * len(bits(topo.mask(helper, core))))
    near = sorted(on + [me])
    marks = {}
    for ps, bs in ((T.PWO, off), (T.PWN, near)):
        for i, b in enumerate(bs):
            marks[bs[0]] = done("ps", g.tensor.matmul(ps[:, i * MS:(i + 1) * MS], T.SEL[0:w1, b * 128:(b + 1) * 128],
                                                      T.DIF[0:w1, :], True, True))
    ofs = {}
    for ps, bs in ((T.PWO, off), (T.PWN, near)):
        wait("v", "ps", marks[bs[0]])
        ofs[bs[0]] = V(g.vector.tensor_scalar(T.OFS[:, bs[0] * MS:(bs[-1] + 1) * MS], ps[:, 0:len(bs) * MS],
                                              float(MID), None, op.add))

    def pick(eng, out, win):
        if eng == "v":
            V(g.vector.tensor_copy(out, win))
        else:
            A(g.scalar.activation(out, win, fn.Identity, bias=T.NZ[:, 0:1]))
        return count["vs"], count["acs"]

    to = landed(me)

    def gather(eng, b, s0, s1):
        if b == me:
            out = T.TW[:, to + s0:to + s1]
        elif s1 == PR:
            out = T.SREL[:, off.index(b), :]
        else:
            out = T.SEND[:, b, s0:s1]
        return pick(eng, out, T.TW[:, 0:R].indirect(T.OFS[:, b * MS + s0 // Q:b * MS + s1 // Q]))

    for q in ("v", "a"):
        wait(q, "vs", ofs[off[0]])
        wait(q, "tl", 32)
    got = {}
    feed = turns(T, topo, me)
    direct = pairs_of(off)
    order = [(feed[0][1], 0, PR), (direct[0], PR, CAPP), (feed[1][1], 0, PR)] + [(bs, PR, CAPP) for bs in direct[1:]]
    for bs, s0, s1 in order:
        for b in bs:
            got[(b, s0)] = gather("va"[off.index(b) % 2], b, s0, s1)
    for q in ("v", "a"):
        wait(q, "vs", ofs[near[0]])
    for i, b in enumerate(on + [me]):
        got[b] = gather("va"[i % 2], b, 0, CAPP)

    def send(marks, items, mask):
        wait("g", "vs", max(m[0] for m in marks))
        wait("g", "acs", max(m[1] for m in marks))
        ms, k = split(mask, len(items))
        g.remote_dma_fused([RemoteDMATransfer(dst_ids=[dst_id(topo, c, core)], dma_engine_mask=m, remote_sem=T.sem[s],
                                              src=a, dst=b) for m, (c, s, a, b) in zip(ms, items)], local_sem=T.sem.sx)
        count["sx"] += k * len(items)

    for j, (c, now) in enumerate(feed):
        i, e, n = off.index(now[0]), dict(mine)[c].index(now[0]), len(now)
        send([got[(b, 0)] for b in now], [(c, "rl%d" % j, T.SREL[:, i:i + n, :], T.RB[:, e:e + n, :])],
             inside if j else inside | outside)
        for bs in direct[j:j + 1]:
            send([got[(b, PR)] for b in bs],
                 [(T.cores[b], "rb%d" % me, T.SEND[:, b, PR:CAPP], T.TW[:, to + PR:to + CAPP]) for b in bs], outside)
    for now in portions(on):
        send([got[b] for b in now],
             [(T.cores[b], "rc%d" % me, T.SEND[:, b, :], T.TW[:, to:to + CAPP]) for b in now], inside)

    arrivals = [("iv", len(bits(topo.mask(helper, core) & ~topo.mask(helper, T.cores[off[0]]))))]
    for a in on:
        o = others(T, topo, a)
        inside_a = topo.mask(T.cores[a], core) & ~topo.mask(T.cores[a], T.cores[o[0][0]])
        run = [p for p in portions(o[1]) if me in p][0]
        arrivals.append(("rc%d" % a, split(inside_a, len(run))[1]))
    for a in off:
        run = [p for p in pairs_of(others(T, topo, a)[0]) if me in p][0]
        arrivals.append(("rb%d" % a, split(topo.mask(T.cores[a], core), len(run))[1]))
        for c, dests in relays(T, topo, a):
            if me in dests:
                arrivals.append(("ra%d" % a, split(topo.mask(c, core), len(dests))[1]))
    wait("v", "acs", count["acs"])
    wait("a", "vs", count["vs"])
    wait("a", "acs", count["acs"])
    vself()
    for q in ("v", "a"):
        for s, k in arrivals:
            wait(q, s, k)
    c = 0
    for i, n in enumerate(YBLOCKS):
        v, s = pick("va"[i % 2], T.YB[:, c:c + n], T.TW[:, 0:WIN].indirect(T.INV[:, c // Q:(c + n) // Q]))
        if i % 2:
            wait("s", "acs", s)
        else:
            wait("s", "vs", v)
        g.sync.dma_start(T.y[:, c:c + n], T.YB[:, c:c + n]).then_inc(T.sem.st, 16)
        c += n
    g.wait_ge(T.sem.sx, count["sx"])
    g.wait_ge(T.sem.sn, sent)
    wait("s", "gs", count["gs"])
    wait("s", "ps", count["ps"])
    g.sync.wait_ge(T.sem.st, 16 * len(YBLOCKS))
